import numpy as np, ml_dtypes
CORES = [2,3,42,43,82,83,122,123]
N = 8
import mx_ref
BF = ml_dtypes.bfloat16
def gcols(t, e):
    v = np.concatenate([t.reshape(8, 16, -1, 4), np.zeros((8, 16, 1, 4), BF)], axis=2)
    return np.ascontiguousarray(np.stack([v[g][:, e[g]] for g in range(8)])).reshape(128, -1)
def tile(rs):
    return np.stack(rs, axis=2).reshape(128, -1).astype(BF)
def pick(q, e):
    c = np.concatenate([q[0].reshape(128, -1, 4), np.zeros((128, 1, 4), np.uint8)], axis=1); s = np.concatenate([q[1], np.ones((16, 1), np.uint8)], axis=1)
    return (np.ascontiguousarray(c[:, e].reshape(128, -1)), np.ascontiguousarray(s[:, e]))
def join(*qs):
    return (np.concatenate([q[0] for q in qs], axis=1), np.concatenate([q[1] for q in qs], axis=1))
def put(q, e, v):
    c, s = q[0].reshape(128, -1, 4).copy(), q[1].copy(); c[:, e] = v[0].reshape(128, -1, 4); s[:, e] = v[1]
    return (c.reshape(128, -1), s)
def pk(c, s):
    return (np.ascontiguousarray(c), mx_ref.live(s))
def emit(q):
    return q[0], q[1]
def packed(v, rng):
    q = [mx_ref.quantize(np.ascontiguousarray(v[r])) for r in range(N)]
    return np.stack([a for a, b in q]), np.stack([mx_ref.plane(b, rng) for a, b in q])
def values_of_codes():
    e, c = np.zeros((128, 128, 4), np.float32), np.zeros((128, 2, 4), np.uint8)
    e[np.arange(128), np.arange(128), 0] = 1
    c[:127, :, 0] = np.arange(256).reshape(2, 128).T[:127]
    return mx_ref.matmul(mx_ref.quantize(e.reshape(128, 512).astype(BF)), (c.reshape(128, 8), np.full((16, 2), 127, np.uint8))).T.reshape(-1).astype(np.float64)
CODE_VALUE, SCALE_VALUE = values_of_codes(), 2.0 ** (np.arange(256) - 127.0)
def decode(q):
    return (CODE_VALUE[q[0]].reshape(16, 8, -1, 4) * SCALE_VALUE[q[1]][:, None, :, None] + 0.0).reshape(128, -1).astype(np.float32)
def f(rng, *shape):
    return mx_ref.flush((rng.standard_normal(shape, dtype=np.float32) * np.exp2(rng.integers(-2, 3, shape[:-1] + (1,)))).astype(BF))
def wide(rng, *shape, cols=0):
    v = rng.standard_normal(shape, dtype=np.float32) * np.exp2(rng.integers(-12, 13, shape)).astype(np.float32)
    if cols: v *= np.repeat(np.exp2(rng.integers(-cols, cols + 1, shape[:-2] + (1, shape[-1] // 4))) * (rng.random(shape[:-2] + (1, shape[-1] // 4)) > 0.0625), 4, axis=-1).astype(np.float32)
    return mx_ref.flush(v.astype(BF))
C, I, ST, M, R = 256, 32, 8, 64, 3
def big(v):
    v = v.astype(np.float32)
    v[np.abs(v) < np.float32(2.0 ** -16)] = 0
    return v.astype(BF)
def numbers_of(rng):
    return {"x": big(f(rng, N, 128, 4 * C)), "u": np.array(f(rng, N, 128, 512)), "v": np.array(f(rng, N, 128, 512))}
def layers(rng):
    return big(f(rng, N, 128, 2048)).reshape(N, 8, 16, 4, 8, 16, 4)
def through(w, some):
    for i in some:
        w[:, :, i] = 0
        w[:, :, :, :, :, i] = 0
        for g in range(8):
            for b in range(4): w[:, g, i, b, g, i, b] = 32
    return w
def weights(rng, w):
    c, p = packed(np.ascontiguousarray(w).reshape(N, 128, 2048), rng)
    return {"wc": c, "ws": p}
def setup_inputs(rng):
    return {**numbers_of(rng), **weights(rng, layers(rng))}
def setup_inputs_ties(rng):
    d = numbers_of(rng)
    x = d["x"].astype(np.float32).reshape(N, 8, 16, C, 4)
    x[:, :, 0] = 0
    x[:, :, 0, :, 0] = rng.integers(0, 3, (N, 8, C))
    x[:, :, 0, :, 1] = 1.125
    some = rng.permutation(8)[:4]
    k = np.exp2(rng.integers(-2, 3, (N, 8, 1, C, 1)))
    k[:, some] = 1
    s = (N, 8, 8, C, 4)
    e = rng.integers(-21, -14, s)
    for j in range(4): e[:, some[j]] = j - 21
    x[:, :, 8:] = (129 + 2 * rng.integers(0, 64, s)) * np.exp2(e) * rng.choice([-1.0, 1.0], s) * k
    x[:, :, 8, :, 0] = 1.96875 * k[:, :, 0, :, 0]
    u = d["u"].reshape(N, 128, 128, 4)
    u[:, :, ::16] = 0
    o = rng.permutation(N)
    for r in range(N):
        for h in range(0, 128, 16):
            if r != o[0]:
                if h // 16 in some: u[r, h + 9:h + 16, h] = rng.choice([-1.0, 1.0], (7, 4)).astype(np.float32).astype(BF)
                else: u[r, h, h, 0] = -1.0 if r == o[1] else 1.0
            for i in (1, 2):
                if r == o[2] or r == o[3]: u[r, :, h + i] = 0
                if r == o[3]: u[r, h, h + i, 1] = 1
    w = through(layers(rng), [0])
    for g in some:
        w[:, :, :, :, g, 8:] = 0
        w[:, g, 0, 0, g, 8, 1] = 56
        for i in range(9, 16):
            for b in range(4): w[:, g, i, b, g, i, b] = 16
    return {"x": x.reshape(N, 128, 4 * C).astype(BF), "u": u.reshape(N, 128, 512), "v": d["v"], **weights(rng, w)}
def setup_inputs_near(rng):
    d = numbers_of(rng)
    x = d["x"].astype(np.float32).reshape(N, 8, 16, C, 4)
    x[:, :, 0] = 0
    x[:, :, 8:] = 0
    c = (rng.permutation(8) % 2 * 2.0 - 1.0)[:, None]
    s = rng.integers(0, 16, (N, 8, C))
    x[:, :, 8] = ((s[:, :, :, None] >> np.arange(4)) & 1) * np.exp2(np.arange(4) - 23.0)
    u = d["u"].reshape(N, 128, 128, 4)
    u[:, :, ::16] = 0
    o = rng.permutation(N) % 4
    for r in range(N):
        if o[r] % 2 == 0:
            x[r, :, 0, :, 0] = c
            x[r, :, 11, :, 0] = 2.0 ** -10
        else:
            for g in rng.permutation(8)[:4]: x[r, g, 0, rng.integers(C), 0] = 2.0 ** 26 * rng.choice([-1.0, 1.0])
        k = 1.0 if o[r] < 2 else 2.0 ** -30
        for h in range(0, 128, 16):
            u[r, h, h, 0] = k
            u[r, h + 8, h] = k
            u[r, h + 11, h, 0] = k
    return {"x": x.reshape(N, 128, 4 * C).astype(BF), "u": u.reshape(N, 128, 512), "v": d["v"], **weights(rng, through(layers(rng), [0, 8, 9, 10, 11, 12, 13, 14, 15]))}
def setup_inputs_huge(rng):
    d = numbers_of(rng)
    o = rng.permutation(N)
    c = rng.choice([-1.0, 1.0], (N, 1, 1, C, 1))
    c[o < N // 2] = (rng.permutation(N // 2) % 2 * 2.0 - 1.0).reshape(-1, 1, 1, 1, 1)
    x = 0.9 * 2.0 ** 30 * c * (0.8 + 0.2 * rng.random((N, 1, 1, C, 1))) * (0.95 + 0.05 * rng.random((N, 8, 16, C, 4)))
    x[:, :, 0] = np.abs(x[:, :, 0])
    x[:, :, 1, :, :2] *= rng.choice([-1.0, 1.0], (N, 8, C, 2))
    u = d["u"].reshape(N, 128, 128, 4)
    a = 2.0 ** 30 * (1.0 - 0.1 * rng.random((N, 8, 16, 8, 4))) * (rng.permutation(8) % 2 * 2.0 - 1.0)[:, None]
    a[:, :, :2] = 0
    u[:, :, ::16] = a.reshape(N, 128, 8, 4).astype(np.float32).astype(BF)
    for h in range(0, 128, 16):
        u[:, :, h + 1:h + 3] = 0
        u[:, h + 1, h + 1, 0] = 1
        u[:, h + 1, h + 2, 1] = 1
    w = np.zeros((N, 128, 4, 128, 4), np.float32)
    i = np.arange(128)
    j = i[i % 16 > 1]
    for r in range(N):
        for b in range(4):
            if o[r] < N // 2: w[r, j - j % 16, b, j, b] = -16.0 * c[r, 0, 0, 0, 0]
            else: w[r, i, b, i, b] = -1
    return {"x": x.astype(np.float32).reshape(N, 128, 4 * C).astype(BF), "u": u.reshape(N, 128, 512), "v": d["v"], **weights(rng, w.astype(BF))}
def setup_inputs_few(rng):
    d = numbers_of(rng)
    x = d["x"].reshape(N, 8, 16, C, 4)
    c = np.where(rng.random((N, 8, C, 2)) < 0.0625, 1.0, -1.0)
    e = rng.permutation(N)
    c[e[1], :, :, 0] = 1
    c[e[1], :, :, 1] = -1
    c[e[2]] = -1
    for g in range(8):
        for b in range(2): c[e[2], g, rng.integers(C), b] = 1
    u = d["u"].reshape(N, 128, 128, 4)
    for h in range(0, 128, 16):
        u[:, :, h + 1:h + 3] = 0
        u[:, h + 1, h + 1, 0] = 1
        u[:, h + 1, h + 2, 1] = 1
    w = layers(rng)
    w[:, :, :, :, :, 1] = 0
    for r in e[1::2]:
        c[r] *= 2.0 ** -28
        x[r, :, :8] = 0
        x[r, :, 2:4, :, 0] = (rng.integers(-2, 3, (8, 1, C)) * 2.0 ** -28).astype(np.float32).astype(BF)
        u[r, :, ::16] = 0
        for h in range(0, 128, 16):
            u[r, h + 1, h + 1, 0] = 2.0 ** -30
            u[r, h + 1, h + 2, 1] = 2.0 ** -30
            u[r, h + 2, h, 0] = 1.875 * 2.0 ** -30
            u[r, h + 3, h, 0] = -1.75 * 2.0 ** -30
        w[r, :, :, :, :, :8] = 0
    x[:, :, 1, :, :2] = c.astype(np.float32).astype(BF)
    x[e[0]] = 0
    return {"x": x.reshape(N, 128, 4 * C), "u": u.reshape(N, 128, 512), "v": d["v"], **weights(rng, w)}
def setup_inputs_spread(rng):
    d = setup_inputs(rng)
    d["x"] = big(wide(rng, N, 128, 4 * C, cols=6))
    return d
def check_inputs(d):
    b = []
    for k in ("x", "u", "v"):
        a = np.abs(d[k].astype(np.float32))
        if not (np.isfinite(a).all() and ((a == 0) | (a >= 2.0 ** -30) & (a <= 2.0 ** 30)).all()): b.append("a value of " + k)
    none, least, most = [emit(mx_ref.quantize(np.full((128, 16), k, np.float32).astype(BF)))[1][0, 0] for k in (0.0, 2.0 ** -30, 2.0 ** 30)]
    for r in range(N):
        if ((d["wc"][r] == 0x7F) | (d["wc"][r] == 0xFF)).any(): b.append("wc: a code that is no number")
        s = mx_ref.live(d["ws"][r])
        if ((s != none) & ((s < least) | (s > most))).any(): b.append("ws: a scale out of range")
    return b
def reference(x, u, v, wc, ws):
    qu = [mx_ref.quantize(u[r]) for r in range(N)]
    lay = [pk(wc[r], ws[r]) for r in range(N)]
    now = [x[r] for r in range(N)]
    k = np.arange(I)
    taken = np.zeros((N, 8, C), np.int64)
    half = np.float32(0.5)
    for t in range(R):
        own, mine, sent = [], [], []
        for r in range(N):
            q = mx_ref.quantize(now[r])
            s = mx_ref.matmul(qu[r], q) + np.float32(0.0)
            own.append(decode(q))
            order = np.argsort(-s[::16], axis=1, kind="stable")
            even, odd = (s[1::16] > 0).astype(np.int64), (s[2::16] > 0).astype(np.int64)
            place = np.zeros((8, C), np.int64)
            np.put_along_axis(place, order, np.arange(C)[None] * np.ones((8, 1), np.int64), axis=1)
            j = place // ST
            n = 2 * j + np.where(j % 2 == 0, even, odd)
            m = 2 * ((j + I - 1) % I) + np.where(j % 2 == 0, odd, even)
            mine.append((np.minimum(n, m), np.maximum(n, m)))
            first, last = np.full((8, M), -1), np.full((8, M), -1)
            for i in range(2 * ST):
                for to, at in ((last, i), (first, 2 * ST - 1 - i)):
                    e = order[:, (ST * k + at) % C]
                    c = np.where(k % 2 == 0, np.take_along_axis(even, e, axis=1), np.take_along_axis(odd, e, axis=1))
                    np.put_along_axis(to, 2 * k + c, e, axis=1)
            a = own[r].astype(BF)
            z = ((gcols(a, first).astype(np.float32) + gcols(a, last).astype(np.float32)) * half).astype(BF).astype(np.float32)
            sent.append(mx_ref.quantize(((z + np.roll(z, -8, axis=1)) * half).astype(BF)))
        for r in range(N):
            q = sent[(r + N - 1) % N]
            h = tile([mx_ref.matmul(pick(lay[r], np.arange(128 * b, 128 * b + 128)), q) * np.float32(0.03125) for b in range(4)])
            w = mx_ref.matmul(qu[r], mx_ref.quantize(h))[::16] + np.float32(0.0)
            lo, hi = mine[r]
            taken[r] = np.where(np.take_along_axis(w, hi, axis=1) > np.take_along_axis(w, lo, axis=1), hi, lo)
            now[r] = (own[r] + gcols(h, taken[r]).astype(np.float32)).astype(BF)
    y, nd = np.zeros((N, 128, C), np.float32), np.zeros((N, 8, C), np.float32)
    oc, osc = np.zeros((N, 128, 4 * C), np.uint8), np.zeros((N, 16, C), np.uint8)
    for r in range(N):
        q = mx_ref.quantize(now[r])
        y[r] = mx_ref.matmul(mx_ref.quantize(v[r]), q)
        nd[r] = taken[r]
        oc[r], osc[r] = emit(q)
    return {"y": y, "nd": nd, "oc": oc, "osc": osc}

@@ -1,0 +1,401 @@
+from concourse.mybir import dt, AluOpType, ActivationFunctionType
+
+A = AluOpType
+F = ActivationFunctionType
+C4, U8, BF, F32, I32, U16 = "float8_e4m3fn_x4", "uint8", "bfloat16", "float32", "int32", "uint16"
+ROUNDS = 3
+NY = 66
+LAND = [142, 76, 10]
+TILES = [(0, 256), (256, 192), (576, 128), (448, 128)]
+
+
+def _s(n, d):
+    return ("sbuf", [128, n], d)
+
+
+SCRATCH = {
+    "ps": ("psum", [128, 4096], F32),
+    "xin": _s(1024, BF), "ut": _s(512, BF), "vt": _s(512, BF), "xs": _s(1024, BF),
+    "qu": _s(128, C4), "su": _s(128, U8), "qp": _s(512, C4), "sp": _s(512, U8),
+    "qv": _s(128, C4), "sv": _s(128, U8), "qw": _s(512, C4), "sw": _s(512, U8),
+    "qx": _s(256, C4), "sx": _s(256, U8), "qe": _s(512, C4), "se": _s(512, U8),
+    "qa": _s(256, C4), "sa": _s(256, U8), "ql": _s(704, C4), "sl": _s(704, U8),
+    "qy": _s(384, C4), "sy": _s(384, U8), "lc": _s(336, C4), "ls": _s(336, U8),
+    "qh": _s(128, C4), "sh": _s(128, U8),
+    "pi": _s(8, I32), "ci": _s(8, I32), "cf": _s(8, F32), "cd": _s(8, F32), "lpi": _s(32, I32), "lpk": _s(32, U16),
+    "a16": _s(288, F32), "g128": _s(128, F32), "d128": _s(128, F32), "jr": _s(256, F32), "jt": _s(256, F32),
+    "m2": _s(34, F32), "msel": _s(34, F32), "alt": _s(272, BF), "nt": _s(192, F32), "zt": _s(512, BF),
+    "mask": _s(256, F32), "d0g": _s(256, F32), "d0d": _s(256, BF), "d0p": _s(256, F32), "d0b": _s(512, BF),
+    "d0r": _s(280, F32), "d0s": _s(280, F32), "eb": _s(520, BF), "bm": _s(128, BF), "wab": _s(1024, BF),
+    "sm": _s(256, F32), "sg": _s(256, F32), "tc": _s(256, BF), "rc": _s(256, F32),
+    "lt": _s(2816, BF), "jk": _s(1920, BF), "rs": _s(16, F32),
+    "ds": _s(256, BF), "pre": _s(32, F32), "hp": _s(256, F32), "lp": _s(16, U16),
+    "xv": _s(256, F32), "xo": _s(288, F32), "na": _s(280, F32), "s1": _s(34, F32), "s2": _s(18, F32),
+    "l1": _s(18, U16), "f2": _s(1056, BF), "gz": _s(544, BF), "zz": _s(544, BF),
+    "yt": _s(512, BF), "eo": _s(512, BF), "eh": _s(512, BF), "wi": _s(48, I32), "wf": _s(192, F32),
+    "lcb": _s(16, U16), "th": _s(256, F32), "ht": _s(512, BF), "hpl": _s(320, BF), "vs": _s(66, F32),
+    "dtb": _s(192, F32), "bt": _s(256, BF), "bh": _s(256, BF), "fa": _s(16, F32), "lh": _s(16, U16),
+    "gh": _s(512, BF), "ndf": _s(256, F32), "yo": _s(256, F32),
+}
+NSEM = 140
+SEMAPHORES = ["s%d" % i for i in range(NSEM)] + ["sent", "arr0", "arr1", "arr2"]
+
+
+def rank_program(g, core, T, topo):
+    rank = T.rank_of(core)
+    if rank is None:
+        return
+    n = len(T.cores)
+    nxt, prv = T.cores[(rank + 1) % n], T.cores[(rank - 1) % n]
+    V, S, P = g.vector, g.scalar, g.tensor
+    queue = {"g": g, "v": V, "a": S, "p": P, "s": g.sync}
+
+    ops, lastw, readers, tags = [], {}, {}, {}
+    know = {q: 0 for q in queue}
+
+    def op(q, tag, fn, r=(), w=(), inc=1, acc=False, ext=None):
+        deps = set()
+        for k in r:
+            if k in lastw:
+                deps.add(lastw[k])
+            if k[0] == "#":
+                deps.update(o for o in readers.get(k, ()) if ops[o]["q"] != q)
+        for k in w:
+            if k in lastw and not acc:
+                deps.add(lastw[k])
+            deps.update(readers.get(k, ()))
+        t = tags.setdefault(tag, {"ops": [], "closed": 0, "sem": len(tags)}) if tag else None
+        waits = [ext] if ext else []
+
+        def need(d):
+            if know[q] >> d & 1:
+                return
+            td = tags[ops[d]["tag"]]
+            td["closed"] = len(td["ops"])
+            waits.append((T.sem["s%d" % td["sem"]], sum(ops[o]["inc"] for o in td["ops"])))
+            for o in td["ops"]:
+                know[q] |= ops[o]["know"] | 1 << o
+        for d in sorted(deps, reverse=True):
+            need(d)
+        if t:
+            for d in t["ops"][:t["closed"]]:
+                need(d)
+        me = len(ops)
+        ops.append({"q": q, "tag": tag, "fn": fn, "inc": inc, "waits": waits, "know": know[q]})
+        if t:
+            t["ops"].append(me)
+        for k in r:
+            readers.setdefault(k, []).append(me)
+        for k in w:
+            lastw[k] = me
+            readers[k] = []
+
+    def bank(b, a=0, e=256, s=1):
+        return T.ps[:, 512 * b + a:512 * b + e:s]
+
+    def ts(tag, out, in0, s1, s2, o0, o1, r, w):
+        if o1 is None:
+            op("v", tag, lambda: V.tensor_scalar(out, in0, s1, None, o0), r, w)
+        else:
+            op("v", tag, lambda: V.tensor_scalar(out, in0, s1, s2, o0, o1), r, w)
+
+    def tt(tag, out, a, b, o, r, w):
+        op("v", tag, lambda: V.tensor_tensor(out, a, b, o), r, w)
+
+    def cp(tag, out, a, r, w):
+        op("v", tag, lambda: V.tensor_copy(out, a), r, w)
+
+    def scan(tag, out, d0, d1, o0, o1, r, w):
+        op("v", tag, lambda: V.tensor_tensor_scan(out, d0, d1, 0.0, o0, o1), r, w)
+
+    def act(tag, out, a, f, r, w, **kw):
+        op("a", tag, lambda: S.activation(out, a, f, **kw), r, w)
+
+    def quant(tag, q, s, a, r, w):
+        op("v", tag, lambda: V.quantize_mx(q, s, a), r, w)
+
+    def mm(tag, out, lq, lsc, rq, rsc, r, w, start=True, stop=True, ext=None):
+        op("p", tag, lambda: P.matmul_mx(out, lq, lsc, rq, rsc, start, stop), r, w, acc=not start, ext=ext)
+
+    def iota(tag, out, pat, base, cm, w, small=True):
+        if small:
+            op("g", tag, lambda: g.iota(out, pat, base, cm, allow_small_or_imprecise_dtypes=True), (), w)
+        else:
+            op("g", tag, lambda: g.iota(out, pat, base, cm), (), w)
+
+    def zero(tag, out, m, w):
+        iota(tag, out, [[0, m]], 0, 0, w)
+
+    def dma(q, tag, out, a, r, w):
+        op(q, tag, lambda: queue[q].dma_start(out, a), r, w, inc=16)
+
+    def col(t, j):
+        return t[:, j:j + 1]
+
+    def side(q, s, b):
+        return q[:, 128 * b:128 * b + 128], s[:, 128 * b:128 * b + 128]
+
+    def pick_codes(tag, a, b):
+        cp(tag, T.qp[:, 16 * a:16 * b].bitcast(dt.uint32), T.qu[:, 0:128].bitcast(dt.uint32).indirect(T.lpk[:, a:b]),
+           ["qu", "lpk%d" % a], ["pc%d" % a])
+
+    def pick_scales(tag, a, b):
+        act(tag, T.sp[:, 16 * a:16 * b], T.su[:, 0:128].indirect(T.lpk[:, a:b]), F.Copy, ["qu", "lpk%d" % a], ["ps%d" % a])
+
+    def column(j, src, sc, bi):
+        act("k4", col(T.cd, j), col(T.cf, src), F.Identity, ["cf"], ["cd%d" % j], scale=sc, bias=bi)
+
+    def apart(tag, out, a, j, r, w):
+        act(tag, out, a, F.Abs, r + ["cf"], w, scale=-1.0, bias=col(T.cf, j))
+
+    def equal(tag, out, a, r, w):
+        act(tag, out, a, F.Relu, r, w, scale=-1.0, bias=1.0)
+
+    dma("a", "ldu", T.ut[:], T.u[:], [], ["ut"])
+    dma("s", "ldx", T.xin[:], T.x[:], [], ["xin"])
+    dma("s", "ldw", T.qw[:].bitcast(dt.uint8), T.wc[:], [], ["qw"])
+    dma("s", "ldw", T.sw[:], T.ws[:], [], ["sw"])
+    dma("s", "ldv", T.vt[:], T.v[:], [], ["vt"])
+
+    iota("i0", T.pi[:], [[0, 8]], 0, 1, ["pi"], False)
+    iota("i3", T.d128[:], [[1, 128]], 0, -1, ["d128"])
+    iota("i1", T.a16[:], [[0, 18], [1, 16]], 0, 0, ["a16"])
+    iota("i2", T.lpi[:], [[1, 2], [1, 2], [16, 8]], 0, 0, ["lpi"], False)
+    iota("i4", T.g128[:], [[16, 8], [0, 16]], 0, 0, ["g128"])
+    zero("i9", T.lt[:, 4 * 208:4 * 256], 192, ["z0"])
+    zero("i9", T.lt[:, 4 * 400:4 * 448], 192, ["z1"])
+    op("v", "k0", lambda: V.memset(T.eb[:], 0.0), (), ["eb"])
+    for j, (sh, m) in enumerate([(0, 15), (0, 112), (0, 8), (0, 4), (1, 1), (0, 1), (3, 1)]):
+        ts("k1", col(T.ci, j), col(T.pi, j), sh, m, A.logical_shift_right, A.bitwise_and, ["pi"], ["ci%d" % j])
+    ts("k6", T.eb[:, 3:515:4], T.d128[:], 0.0, None, A.is_equal, None, ["d128"], ["eb"])
+    cp("k2", T.cf[:, 0:7], T.ci[:, 0:7], ["ci%d" % j for j in range(7)], ["cf"])
+    for b in range(4):
+        quant("k12", *side(T.qe, T.se, b), T.eb[:, 3 - b:515 - b], ["eb"], ["qe%d" % b])
+    ts("k7", T.mask[:], T.a16[:, 0:256], col(T.cf, 0), None, A.is_equal, None, ["a16", "cf"], ["mask"])
+    cp("k5", T.lpk[:, 0:8], T.lpi[:, 0:8], ["lpi"], ["lpk0"])
+    ts("k5", T.lpk[:, 8:16], T.lpi[:, 8:16], col(T.cf, 6), None, A.add, None, ["lpi", "cf"], ["lpk8"])
+    cp("k5", T.lpk[:, 16:32], T.lpi[:, 16:32], ["lpi"], ["lpk16"])
+    column(2, 3, 2.0 ** 22, -2.0 ** 23)
+    column(3, 3, -2.0 ** 21, 2.0 ** 22)
+    column(5, 0, -511.0, 7664.0)
+    column(1, 4, 257.0, 0.0)
+    column(0, 5, -4096.0, 2048.0)
+    act("k8", T.d0g[:], T.a16[:, 0:256], F.Sign, ["a16"], ["d0g"])
+    apart("k20", T.d0r[:], T.a16[:, 0:280], 2, ["a16"], ["d0r"])
+    apart("k9", T.bm[:], T.g128[:], 1, ["g128"], ["bm"])
+    quant("k13", T.qu[:], T.su[:], T.ut[:], ["ut"], ["qu"])
+    equal("k3", T.wab[:, 1:512:4], T.bm[:], ["bm"], ["wab1"])
+    pick_codes("k14", 0, 8)
+    pick_scales("k15", 0, 8)
+    op("g", "k10", lambda: g.affine_select(T.wab[:, 0:512:4], T.wab[:, 1:512:4], [[1, 128]], A.is_gt, 0.0, 0, -1), ["wab1"], ["wab0"])
+    iota("i5", T.jr[:], [[1, 256]], 2 ** 20 + 1, 0, ["jr"])
+    zero("i10", T.lt[:, 4 * 464:4 * 576], 448, ["z3"])
+    zero("i11", T.lt[:, 4 * 656:4 * 704], 192, ["z2"])
+    zero("i6", T.rs[:, 0:1], 1, ["rs0"])
+    iota("i6", T.m2[:], [[0, 17], [8, 2]], -6, 0, ["m2"])
+    zero("i7", T.f2[:, 0:258:257], 2, ["f2y"])
+    zero("i7", T.f2[:, 528:786:257], 2, ["f2z"])
+    iota("i7", T.alt[:], [[0, 136], [1, 2]], 0, 0, ["alt"])
+    zero("i7", T.yt[:, 264:512], 248, ["ytz"])
+    zero("i8", T.zt[:], 512, ["zt"])
+    zero("i8", T.ht[:, 264:512], 248, ["htz"])
+    zero("i8", T.dtb[:], 192, ["d1", "d2", "d3"])
+    iota("i8", T.nt[:], [[0, 3], [1, 64]], 0, 0, ["nt"])
+
+    slot = {t: ((16 - t) // 4, (16 - t) % 4) for t in range(1, 16)}
+
+    def lview(t):
+        j, e = slot[t]
+        return T.lt[:, 4 * TILES[j][0] + e:4 * TILES[j][0] + 64 * t:4]
+
+    def lkeys(j):
+        return ["l%d" % t for t in slot if slot[t][0] == j] + (["l0"] if j == 0 else [])
+
+    def wf(j, m=1):
+        return T.wf[:, 16 * j:16 * (j + m)]
+
+    def wi(j):
+        return T.wi[:, 16 * j:16 * j + 16]
+
+    def cmp(*blocks):
+        for t in blocks:
+            ts("c%d_" % blocks[0], lview(t), bank(0, 0, 16 * t), col(T.sg, 16 * t + 15), None, A.is_lt, None,
+               ["#0", "sg", "z%d" % slot[t][0]], ["l%d" % t])
+        for t in blocks:
+            act("rs", T.jk[:, 8 * t * (t - 1):8 * t * (t + 1)], lview(t), F.Identity, ["l%d" % t], ["rs%d" % t, "jk%d" % t],
+                scale=-1.0, bias=1.0, accum_out=col(T.rs, t))
+
+    def pack(tag, c, e, keys):
+        quant(tag, T.ql[:, c:e], T.sl[:, c:e], T.lt[:, 4 * c:4 * e], keys, [tag])
+
+    def count(j, tag):
+        c, m = TILES[j]
+        mm("mp", bank(3, 0, m), *side(T.qa, T.sa, min(j, 1)), T.ql[:, c:c + m], T.sl[:, c:c + m], [tag, "qa"], ["#3"],
+           start=j == 0, stop=j == 2)
+
+    qx, sx = T.qx[:], T.sx[:]
+    rid, pid = topo.addr(nxt)[:2]
+
+    def colours():
+        for j in range(2):
+            mm("me%d" % j, bank(j), *side(T.qp, T.sp, 2 + j), qx, sx, ["qx", "pc16", "ps16"], ["#%d" % j])
+            act("eo", T.eo[:, 256 * j:256 * j + 256], bank(j), F.Sign, ["#%d" % j], ["eo%d" % j])
+
+    for k in range(ROUNDS):
+        first, last = k == 0, k == ROUNDS - 1
+        if first:
+            quant("qx", qx, sx, T.xin[:], ["xin"], ["qx"])
+        mm("m0", bank(0), *side(T.qp, T.sp, 0), qx, sx, ["qx", "pc0", "ps0"], ["#0"])
+        if first:
+            pick_codes("k16", 8, 16)
+            pick_scales("k18", 8, 16)
+            pick_codes("k23", 16, 32)
+        mm("m2", bank(2), *side(T.qp, T.sp, 1), qx, sx, ["qx", "pc8", "ps8"], ["#2"])
+        for b in range(4):
+            mm("mf", bank(4 + b), *side(T.qe, T.se, b), qx, sx, ["qx", "qe%d" % b], ["#%d" % (4 + b)])
+        if first:
+            for j in range(2, 8):
+                equal("k11", T.wab[:, 512 * (j // 4) + j % 4:512 * (j // 4) + 512:4], T.bm[:], ["bm"], ["wab%d" % j])
+            equal("k25", T.d0d[:], T.mask[:], ["mask"], ["d0d"])
+        tt("sm", T.sm[:], bank(0), T.mask[:], A.mult, ["#0", "mask"], ["sm"])
+        scan("sg", T.sg[:], T.d0g[:], T.sm[:], A.mult, A.add, ["d0g", "sm"], ["sg"])
+        act("c1", T.tc[:], bank(2), F.Sign, ["#2"], ["tc"])
+        if first:
+            act("k19", T.d0p[:], T.mask[:], F.Identity, ["mask"], ["d0p"], scale=-66048.0, bias=512.0)
+            act("k26", T.jt[:], T.jr[:], F.Identity, ["jr", "cd1"], ["jt"], bias=col(T.cd, 1))
+        act("c2", T.rc[:], T.tc[:], F.Relu, ["tc", "cd2", "cd3"], ["rc"], scale=col(T.cd, 2), bias=col(T.cd, 3))
+        cmp(15)
+        cmp(14, 13)
+        cmp(12, 11)
+        tt("dg", T.lt[:, 0:1024:4], bank(0), T.sg[:], A.is_le, ["#0", "sg", "z0"], ["l0"])
+        cmp(10, 9)
+        if first:
+            quant("k17", T.qa[:], T.sa[:], T.wab[:], ["wab%d" % j for j in range(8)], ["qa"])
+        pack("qla", 0, 256, lkeys(0))
+        count(0, "qla")
+        cmp(4, 3, 2, 1)
+        scan("ds", T.ds[:], T.d0d[:], T.lt[:, 0:1024:4], A.mult, A.add, ["d0d", "l0"], ["ds"])
+        pack("qlb", 256, 576 if first else 512, lkeys(1) + lkeys(3))
+        count(1, "qlb")
+        count(3, "qlb")
+        cmp(8, 7)
+        cmp(6, 5)
+        ts("dc", T.pre[:, 0:16], T.ds[:, 15:256:16], col(T.cd, 5), None, A.add, None, ["ds", "cd5"], ["dc"])
+        pack("qlc", 576, 704, lkeys(2))
+        count(2, "qlc")
+        scan("xv", T.xv[:], T.jt[:], T.rc[:], A.max, A.min, ["jt", "rc"], ["xv"])
+        if first:
+            ts("k21", T.msel[:], T.m2[:], col(T.cf, 2), 2.0 ** 21, A.subtract, A.mult, ["m2", "cf"], ["msel"])
+            equal("k22", T.d0r[:], T.d0r[:], ["d0r"], ["d0r"])
+            act("k24", T.d0s[:], T.d0r[:], F.Identity, ["d0r", "cd0"], ["d0s"], scale=-2.0 ** 25, bias=col(T.cd, 0))
+        scan("hp", T.hp[:], T.d0p[:], bank(3), A.add, A.max, ["d0p", "#3"], ["hp"])
+        tt("pre", T.pre[:, 16:32], T.rs[:], T.pre[:, 0:16], A.subtract, ["dc"] + ["rs%d" % t for t in range(16)], ["pre"])
+        tt("lp", T.lp[:], T.hp[:, 15:256:16], T.pre[:, 16:32], A.add, ["hp", "pre"], ["lp"])
+        for b in (0, 2, 1, 3):
+            o = 528 * (b % 2) + 1 + 257 * (b // 2)
+            act("f%d" % (b % 2), T.f2[:, o:o + 256], bank(4 + b), F.Copy, ["#%d" % (4 + b)], ["f%d" % b])
+        if not first:
+            colours()
+        cp("xo", T.xo[:, 0:256].indirect(T.lp[:]), T.xv[:], ["lp", "xv"], ["xo"])
+        ts("w0", wi(0), T.lp[:], 248.0, None, A.add, None, ["lp"], ["w0"])
+        cp("xw", T.xo[:, 256:280], T.xo[:, 0:24], ["xo"], ["xw"])
+        ts("w1", wi(1), wi(0), 2, 62, A.logical_shift_right, A.bitwise_and, ["w0"], ["w1"])
+        scan("na", T.na[:], T.d0s[:], T.xo[:, 0:280], A.add, A.max, ["d0s", "xo", "xw"], ["na"])
+        ts("w2", wi(2), wi(0), 3, 1, A.logical_shift_right, A.bitwise_and, ["w0"], ["w2"])
+        scan("s1", T.s1[:], T.msel[:], T.na[:, 15:280:8], A.add, A.max, ["na", "msel"], ["s1"])
+        ts("w3", wf(0), wi(2), -2.0, 1.0, A.mult, A.add, ["w2"], ["sgn"])
+        ts("s2", T.s2[:, 0:17], T.s1[:, 1:34:2], 1.5 * 2.0 ** 34, 1.5 * 2.0 ** 34, A.add, A.subtract, ["s1"], ["s2"])
+        tt("l1", T.l1[:, 0:17], T.s1[:, 1:34:2], T.s2[:, 0:17], A.subtract, ["s1", "s2"], ["l1"])
+        act("g1", T.gz[:, 272:544], T.f2[:, 528:1042].indirect(T.l1[:, 0:17]), F.Copy, ["l1", "f1", "f3", "f2z"], ["g1"], scale=0.25)
+        if first:
+            pick_scales("k27", 16, 32)
+            column(4, 0, -4.0, 60.0)
+            colours()
+        ts("g0", T.gz[:, 0:272], T.f2[:, 0:514].indirect(T.l1[:, 0:17]), 0.25, None, A.mult, None, ["l1", "f0", "f2", "f2y"], ["g0"])
+        for w in range(2):
+            o = 272 * w
+            scan("zz%d" % w, T.zz[:, o:o + 272], T.alt[:], T.gz[:, o:o + 272], A.mult, A.add, ["alt", "g%d" % w], ["zz%d" % w])
+        for w in range(2):
+            o = 272 * w
+            tt("y", T.yt[:, w:264:2], T.zz[:, o + 1:o + 264:2], T.zz[:, o + 9:o + 272:2], A.add, ["zz%d" % w], ["y%d" % w])
+        quant("qy", *side(T.qy, T.sy, k), T.yt[:], ["y0", "y1", "ytz"], ["qy%d" % k])
+        a, c = LAND[k], 128 * k
+        arr = T.sem["arr%d" % k]
+        op("g", None, lambda a=a, c=c, arr=arr: g.remote_dma(
+            T.lc[:, a:a + NY].bitcast(dt.uint8), T.qy[:, c:c + NY].bitcast(dt.uint8), arr, T.sem.sent, pid, rid, topo.mask(core, nxt)), ["qy%d" % k])
+        op("g", None, lambda a=a, c=c, arr=arr: g.remote_dma(
+            T.ls[:, a:a + NY], T.sy[:, c:c + NY], arr, T.sem.sent, pid, rid, topo.mask(core, nxt)), [])
+        if first:
+            quant("k28", T.lc[:, 208:336], T.ls[:, 208:336], T.zt[:], ["zt"], ["lz"])
+            for j in range(2):
+                ts("k29", T.d0b[:, 256 * j:256 * j + 256], T.mask[:], -260.0, 4.0, A.mult, A.add, ["mask"], ["d0b%d" % j])
+        scan("eh", T.eh[:], T.d0b[:], T.eo[:], A.add, A.max, ["d0b0", "d0b1", "eo0", "eo1"], ["eh"])
+        if k == 1:
+            quant("k30", T.qv[:], T.sv[:], T.vt[:], ["vt"], ["qv"])
+        ts("w4", wf(1, 2), T.eh[:, 15:512:16], col(T.cd, 4), 0.0, A.subtract, A.is_gt, ["eh", "cd4"], ["e", "o"])
+        tt("w5", wf(3), wf(2), wf(1), A.subtract, ["e", "o"], ["dd"])
+        tt("w5", wf(4), wf(1), wi(1), A.add, ["e", "w1"], ["t1"])
+        tt("w6", wf(5), wf(3), wf(0), A.mult, ["dd", "sgn"], ["u"])
+        tt("w6", wf(6), wf(3), wi(2), A.mult, ["dd", "w2"], ["q"])
+        ts("w7", wf(8), wf(5), 64.0, 64.0, A.mult, A.add, ["u"], ["t2"])
+        tt("w7", wf(7), wf(4), wf(6), A.add, ["t1", "q"], ["m"])
+        ts("w8", wf(9), wf(5), 2.0, None, A.add, None, ["u"], ["dl"])
+        tt("w9", T.lcb[:], wf(8), wf(7), A.add, ["t2", "m"], ["lcb"])
+        got = (arr, 2 * len(topo.engines(prv, core)))
+        for b in range(4):
+            mm("mr%d" % b, bank(b, 0, 128), *side(T.qw, T.sw, b), T.lc[:, a:a + 128], T.ls[:, a:a + 128], ["qw", "sw", "lz"], ["#%d" % b],
+               ext=got if b == 0 else None)
+        ts("w10", wf(10), wf(9), col(T.cd, 4), None, A.mult, None, ["dl", "cd4"], ["cl"])
+        for b in range(4):
+            if b % 2 == 0:
+                act("ha", T.ht[:, b:264:4], bank(b, 0, NY), F.Copy, ["#%d" % b], ["h%d" % b], scale=0.03125)
+            else:
+                ts("hv", T.ht[:, b:264:4], bank(b, 0, NY), 0.03125, None, A.mult, None, ["#%d" % b], ["h%d" % b])
+        quant("qh", T.qh[:], T.sh[:], T.ht[:], ["h0", "h1", "h2", "h3", "htz"], ["qh"])
+        tt("w11", wf(11), wf(7), wf(10), A.subtract, ["m", "cl"], ["lo"])
+        act("th", T.th[:], T.nt[:, 0:192].indirect(T.lcb[:]), F.Relu, ["lcb", "nt"], ["th"], scale=2.0 ** -100, bias=-61.5 * 2.0 ** -100)
+        for b in range(4):
+            act("hq", T.hpl[:, 80 * b:80 * b + NY], T.ht[:, b:264:4], F.Copy, ["h%d" % b], ["hq%d" % b])
+        mm("mv", bank(4, 0, 128), *side(T.qp, T.sp, 0), T.qh[:], T.sh[:], ["qh"], ["#4"])
+        cp("vs", T.vs[:], bank(4, 0, NY), ["#4"], ["vs"])
+        tt("d", T.dtb[:, 1:64:2], T.vs[:, 1:64:2], bank(4, 2, 65, 2), A.subtract, ["#4", "vs"], ["d1"])
+        tt("d", T.dtb[:, 64:128], T.vs[:, 0:64], bank(4, 2, 66), A.subtract, ["#4", "vs"], ["d2"])
+        tt("d", T.dtb[:, 128:192:2], T.vs[:, 0:63:2], bank(4, 3, 66, 2), A.subtract, ["#4", "vs"], ["d3"])
+        tt("bt", T.bt[:], T.dtb[:, 0:192].indirect(T.lcb[:]), T.th[:], A.is_lt, ["d1", "d2", "d3", "lcb", "th"], ["bt"])
+        scan("bh", T.bh[:], T.d0b[:, 0:256], T.bt[:], A.add, A.max, ["bt"], ["bh"])
+        tt("fa", T.fa[:], T.bh[:, 15:256:16], wf(9), A.mult, ["bh", "dl"], ["fa"])
+        tt("lh", T.lh[:], T.fa[:], wf(11), A.add, ["fa", "lo"], ["lh"])
+        for b in (2, 3):
+            act("gh%d" % b, T.gh[:, 256 * (b - 2):256 * (b - 1)], T.hpl[:, 80 * b:80 * b + NY].indirect(T.lh[:]), F.Copy,
+                ["lh", "hq%d" % b], ["gh%d" % b])
+        for b in (0, 1):
+            tt("x", T.xs[:, b:1024:4], T.hpl[:, 80 * b:80 * b + NY].indirect(T.lh[:]), T.f2[:, 528 * b + 1:528 * b + 257], A.add,
+               ["lh", "hq%d" % b, "f%d" % b], ["x%d" % b])
+        for b in (2, 3):
+            tt("x", T.xs[:, b:1024:4], bank(4 + b), T.gh[:, 256 * (b - 2):256 * (b - 1)], A.add, ["#%d" % (4 + b), "gh%d" % b], ["x%d" % b])
+        if last:
+            act("nd", T.ndf[:], T.nt[:, 0:128].indirect(T.lh[:]), F.Copy, ["lh", "nt"], ["ndf"])
+            dma("s", "out", T.nd[:], T.ndf[0:128:16, :], ["ndf"], ["o0"])
+        quant("qx", qx, sx, T.xs[:], ["x0", "x1", "x2", "x3"], ["qx"])
+
+    for j in range(2):
+        mm("m%d" % (2 * j), bank(2 * j, 0, 128), T.qv[:], T.sv[:], *side(T.qx, T.sx, j), ["qx", "qv"], ["#%d" % (2 * j)])
+    dma("s", "out", T.oc[:], T.qx[:].bitcast(dt.uint8), ["qx"], ["o1"])
+    for j in range(4):
+        dma("as"[j % 2], "out", T.osc[4 * j:4 * j + 4, :], T.sx[32 * j:32 * j + 4, :], ["qx"], ["o%d" % (2 + j)])
+    cp("yo", T.yo[:, 0:128], bank(0, 0, 128), ["#0"], ["yo0"])
+    dma("s", "out", T.y[:, 0:128], T.yo[:, 0:128], ["yo0"], ["o6"])
+    act("c1", T.yo[:, 128:256], bank(2, 0, 128), F.Copy, ["#2"], ["yo1"])
+    dma("a", "out", T.y[:, 128:256], T.yo[:, 128:256], ["yo1"], ["o7"])
+    op("g", None, None, ["o%d" % j for j in range(8)], ext=(T.sem.sent, 2 * ROUNDS * len(topo.engines(core, nxt))))
+
+    assert len(tags) <= NSEM
+    for i, o in enumerate(ops):
+        for sem, val in o["waits"]:
+            queue[o["q"]].wait_ge(sem, val)
+        if o["fn"] is None:
+            continue
+        ins = o["fn"]()
+        t = tags.get(o["tag"])
+        if t and i in t["ops"][:t["closed"]]:
+            ins.then_inc(T.sem["s%d" % t["sem"]], o["inc"])

@@ -5,8 +5,10 @@ F = ActivationFunctionType
 C4, U8, BF, F32, I32, U16 = "float8_e4m3fn_x4", "uint8", "bfloat16", "float32", "int32", "uint16"
 ROUNDS = 3
 NY = 66
+NA = 128
 LAND = [142, 76, 10]
 TILES = [(0, 256), (256, 192), (576, 128), (448, 128)]
+TINY, BIG = 2.0 ** -100, 2.0 ** 90
 
 
 def _s(n, d):
@@ -19,23 +21,26 @@ SCRATCH = {
     "qu": _s(128, C4), "su": _s(128, U8), "qp": _s(512, C4), "sp": _s(512, U8),
     "qv": _s(128, C4), "sv": _s(128, U8), "qw": _s(512, C4), "sw": _s(512, U8),
     "qx": _s(256, C4), "sx": _s(256, U8), "qe": _s(512, C4), "se": _s(512, U8),
-    "qa": _s(256, C4), "sa": _s(256, U8), "ql": _s(704, C4), "sl": _s(704, U8),
+    "qa": _s(128, C4), "sa": _s(128, U8), "ql": _s(704, C4), "sl": _s(704, U8),
     "qy": _s(384, C4), "sy": _s(384, U8), "lc": _s(336, C4), "ls": _s(336, U8),
     "qh": _s(128, C4), "sh": _s(128, U8),
-    "pi": _s(8, I32), "ci": _s(8, I32), "cf": _s(8, F32), "cd": _s(8, F32), "lpi": _s(32, I32), "lpk": _s(32, U16),
-    "a16": _s(288, F32), "g128": _s(128, F32), "d128": _s(128, F32), "jr": _s(256, F32), "jt": _s(256, F32),
+    "pi": _s(8, I32), "ci": _s(8, I32), "cf": _s(8, F32), "cd": _s(16, F32), "lpi": _s(24, I32), "lpk": _s(32, U16),
+    "a16": _s(128, F32), "a16w": _s(288, F32), "a4": _s(128, F32), "gv": _s(128, F32), "d128": _s(128, F32),
+    "jr": _s(256, F32), "jt": _s(256, F32), "kt": _s(16, F32),
     "m2": _s(34, F32), "msel": _s(34, F32), "alt": _s(272, BF), "nt": _s(192, F32), "zt": _s(512, BF),
-    "mask": _s(256, F32), "d0g": _s(256, F32), "d0d": _s(256, BF), "d0p": _s(256, F32), "d0b": _s(512, BF),
-    "d0r": _s(280, F32), "d0s": _s(280, F32), "eb": _s(520, BF), "bm": _s(128, BF), "wab": _s(1024, BF),
-    "sm": _s(256, F32), "sg": _s(256, F32), "tc": _s(256, BF), "rc": _s(256, F32),
+    "own": _s(128, F32), "d0g": _s(128, F32), "d0d": _s(128, BF), "d0p": _s(128, F32), "d0b": _s(128, BF),
+    "d0c": _s(128, BF), "d0l": _s(128, F32), "d0s": _s(280, F32), "eb": _s(520, BF), "wab": _s(512, BF),
+    "tb": _s(544, F32), "tbh": _s(544, F32), "lw": _s(34, U16), "ptab": _s(192, F32), "ndt": _s(384, F32),
+    "sm": _s(256, F32), "sg": _s(256, F32), "tc": _s(256, BF), "sgn": _s(1920, BF),
     "lt": _s(2816, BF), "jk": _s(1920, BF), "rs": _s(16, F32),
     "ds": _s(256, BF), "pre": _s(32, F32), "hp": _s(256, F32), "lp": _s(16, U16),
-    "xv": _s(256, F32), "xo": _s(288, F32), "na": _s(280, F32), "s1": _s(34, F32), "s2": _s(18, F32),
-    "l1": _s(18, U16), "f2": _s(1056, BF), "gz": _s(544, BF), "zz": _s(544, BF),
-    "yt": _s(512, BF), "eo": _s(512, BF), "eh": _s(512, BF), "wi": _s(48, I32), "wf": _s(192, F32),
-    "lcb": _s(16, U16), "th": _s(256, F32), "ht": _s(512, BF), "hpl": _s(320, BF), "vs": _s(66, F32),
-    "dtb": _s(192, F32), "bt": _s(256, BF), "bh": _s(256, BF), "fa": _s(16, F32), "lh": _s(16, U16),
-    "gh": _s(512, BF), "ndf": _s(256, F32), "yo": _s(256, F32),
+    "xv": _s(256, F32), "xo": _s(256, F32), "na": _s(280, F32), "s1": _s(34, F32), "s2": _s(18, F32),
+    "l1": _s(18, U16), "f2": _s(1056, BF), "fi": _s(4 * NA, BF), "gz": _s(544, BF), "zz": _s(544, BF),
+    "yt": _s(512, BF), "eo": _s(512, BF), "eh": _s(512, BF), "wi": _s(48, I32), "wf": _s(128, F32),
+    "lcb": _s(16, U16), "th": _s(256, F32), "lob": _s(256, F32), "l4": _s(256, F32), "lo4": _s(64, F32),
+    "ht": _s(512, BF), "hw": _s(544, BF), "vs": _s(66, F32),
+    "dtb": _s(192, F32), "bt": _s(256, BF), "bh": _s(256, BF), "b16": _s(256, BF), "lh": _s(64, U16), "ln": _s(16, U16),
+    "gh": _s(1024 - 4 * NA, BF), "ndf": _s(256, F32), "yo": _s(256, F32),
 }
 NSEM = 140
 SEMAPHORES = ["s%d" % i for i in range(NSEM)] + ["sent", "arr0", "arr1", "arr2"]
@@ -64,15 +69,15 @@ def rank_program(g, core, T, topo):
             if k in lastw and not acc:
                 deps.add(lastw[k])
             deps.update(readers.get(k, ()))
-        t = tags.setdefault(tag, {"ops": [], "closed": 0, "sem": len(tags)}) if tag else None
-        waits = [ext] if ext else []
+        t = tags.setdefault(tag, {"ops": [], "closed": 0}) if tag else None
+        waits = []
 
         def need(d):
             if know[q] >> d & 1:
                 return
             td = tags[ops[d]["tag"]]
             td["closed"] = len(td["ops"])
-            waits.append((T.sem["s%d" % td["sem"]], sum(ops[o]["inc"] for o in td["ops"])))
+            waits.append((ops[d]["tag"], sum(ops[o]["inc"] for o in td["ops"])))
             for o in td["ops"]:
                 know[q] |= ops[o]["know"] | 1 << o
         for d in sorted(deps, reverse=True):
@@ -81,7 +86,7 @@ def rank_program(g, core, T, topo):
             for d in t["ops"][:t["closed"]]:
                 need(d)
         me = len(ops)
-        ops.append({"q": q, "tag": tag, "fn": fn, "inc": inc, "waits": waits, "know": know[q]})
+        ops.append({"q": q, "tag": tag, "fn": fn, "inc": inc, "waits": waits, "ext": ext, "know": know[q]})
         if t:
             t["ops"].append(me)
         for k in r:
@@ -132,75 +137,101 @@ def rank_program(g, core, T, topo):
     def col(t, j):
         return t[:, j:j + 1]
 
+    def part(t, h, m=128):
+        return t[:, m * h:m * h + m]
+
     def side(q, s, b):
-        return q[:, 128 * b:128 * b + 128], s[:, 128 * b:128 * b + 128]
+        return part(q, b), part(s, b)
 
-    def pick_codes(tag, a, b):
-        cp(tag, T.qp[:, 16 * a:16 * b].bitcast(dt.uint32), T.qu[:, 0:128].bitcast(dt.uint32).indirect(T.lpk[:, a:b]),
-           ["qu", "lpk%d" % a], ["pc%d" % a])
+    def pick_list(b):
+        return part(T.lpk, [0, 3, 1, 2][b], 8)
 
-    def pick_scales(tag, a, b):
-        act(tag, T.sp[:, 16 * a:16 * b], T.su[:, 0:128].indirect(T.lpk[:, a:b]), F.Copy, ["qu", "lpk%d" % a], ["ps%d" % a])
+    def pick_codes(tag, b):
+        cp(tag, part(T.qp, b).bitcast(dt.uint32), T.qu[:, 0:128].bitcast(dt.uint32).indirect(pick_list(b)),
+           ["qu", "lpk%d" % b], ["pc%d" % b])
 
-    def column(j, src, sc, bi):
-        act("k4", col(T.cd, j), col(T.cf, src), F.Identity, ["cf"], ["cd%d" % j], scale=sc, bias=bi)
+    def pick_scales(tag, b):
+        act(tag, part(T.sp, b), T.su[:, 0:128].indirect(pick_list(b)), F.Copy, ["qu", "lpk%d" % b], ["ps%d" % b])
 
-    def apart(tag, out, a, j, r, w):
-        act(tag, out, a, F.Abs, r + ["cf"], w, scale=-1.0, bias=col(T.cf, j))
+    def column(tag, j, src, sc, bi):
+        if isinstance(bi, int):
+            act(tag, col(T.cd, j), col(T.cf, src), F.Identity, ["cf", "cd%d" % bi], ["cd%d" % j], scale=sc, bias=col(T.cd, bi))
+        else:
+            act(tag, col(T.cd, j), col(T.cf, src), F.Identity, ["cf"], ["cd%d" % j], scale=sc, bias=bi)
 
-    def equal(tag, out, a, r, w):
-        act(tag, out, a, F.Relu, r, w, scale=-1.0, bias=1.0)
+    def hold(tag, out, d0, a, h, r, w):
+        scan(tag, part(out, h), d0[:], part(a, h), A.add, A.max, r, w)
 
     dma("a", "ldu", T.ut[:], T.u[:], [], ["ut"])
-    dma("s", "ldx", T.xin[:], T.x[:], [], ["xin"])
+    for h in range(2):
+        dma("s", "ldx%d" % h, part(T.xin, h, 512), part(T.x, h, 512), [], ["xin%d" % h])
     dma("s", "ldw", T.qw[:].bitcast(dt.uint8), T.wc[:], [], ["qw"])
     dma("s", "ldw", T.sw[:], T.ws[:], [], ["sw"])
     dma("s", "ldv", T.vt[:], T.v[:], [], ["vt"])
 
+    R, PAR8, COL4, PAIR2, LAST = range(5)
     iota("i0", T.pi[:], [[0, 8]], 0, 1, ["pi"], False)
-    iota("i3", T.d128[:], [[1, 128]], 0, -1, ["d128"])
-    iota("i1", T.a16[:], [[0, 18], [1, 16]], 0, 0, ["a16"])
-    iota("i2", T.lpi[:], [[1, 2], [1, 2], [16, 8]], 0, 0, ["lpi"], False)
-    iota("i4", T.g128[:], [[16, 8], [0, 16]], 0, 0, ["g128"])
-    zero("i9", T.lt[:, 4 * 208:4 * 256], 192, ["z0"])
-    zero("i9", T.lt[:, 4 * 400:4 * 448], 192, ["z1"])
-    op("v", "k0", lambda: V.memset(T.eb[:], 0.0), (), ["eb"])
-    for j, (sh, m) in enumerate([(0, 15), (0, 112), (0, 8), (0, 4), (1, 1), (0, 1), (3, 1)]):
-        ts("k1", col(T.ci, j), col(T.pi, j), sh, m, A.logical_shift_right, A.bitwise_and, ["pi"], ["ci%d" % j])
-    ts("k6", T.eb[:, 3:515:4], T.d128[:], 0.0, None, A.is_equal, None, ["d128"], ["eb"])
-    cp("k2", T.cf[:, 0:7], T.ci[:, 0:7], ["ci%d" % j for j in range(7)], ["cf"])
-    for b in range(4):
-        quant("k12", *side(T.qe, T.se, b), T.eb[:, 3 - b:515 - b], ["eb"], ["qe%d" % b])
-    ts("k7", T.mask[:], T.a16[:, 0:256], col(T.cf, 0), None, A.is_equal, None, ["a16", "cf"], ["mask"])
-    cp("k5", T.lpk[:, 0:8], T.lpi[:, 0:8], ["lpi"], ["lpk0"])
-    ts("k5", T.lpk[:, 8:16], T.lpi[:, 8:16], col(T.cf, 6), None, A.add, None, ["lpi", "cf"], ["lpk8"])
-    cp("k5", T.lpk[:, 16:32], T.lpi[:, 16:32], ["lpi"], ["lpk16"])
-    column(2, 3, 2.0 ** 22, -2.0 ** 23)
-    column(3, 3, -2.0 ** 21, 2.0 ** 22)
-    column(5, 0, -511.0, 7664.0)
-    column(1, 4, 257.0, 0.0)
-    column(0, 5, -4096.0, 2048.0)
-    act("k8", T.d0g[:], T.a16[:, 0:256], F.Sign, ["a16"], ["d0g"])
-    apart("k20", T.d0r[:], T.a16[:, 0:280], 2, ["a16"], ["d0r"])
-    apart("k9", T.bm[:], T.g128[:], 1, ["g128"], ["bm"])
-    quant("k13", T.qu[:], T.su[:], T.ut[:], ["ut"], ["qu"])
-    equal("k3", T.wab[:, 1:512:4], T.bm[:], ["bm"], ["wab1"])
-    pick_codes("k14", 0, 8)
-    pick_scales("k15", 0, 8)
-    op("g", "k10", lambda: g.affine_select(T.wab[:, 0:512:4], T.wab[:, 1:512:4], [[1, 128]], A.is_gt, 0.0, 0, -1), ["wab1"], ["wab0"])
+    iota("i1", T.d128[:], [[1, 128]], 0, -1, ["d128"])
+    iota("i3", T.lpi[:], [[8, 3], [128, 8]], 0, 0, ["lpi"], False)
+    iota("i4", T.a16[:], [[0, 8], [1, 16]], 0, 0, ["a16"])
+    iota("i2", T.gv[:], [[16, 8], [0, 16]], 0, -1, ["gv"])
     iota("i5", T.jr[:], [[1, 256]], 2 ** 20 + 1, 0, ["jr"])
-    zero("i10", T.lt[:, 4 * 464:4 * 576], 448, ["z3"])
-    zero("i11", T.lt[:, 4 * 656:4 * 704], 192, ["z2"])
-    zero("i6", T.rs[:, 0:1], 1, ["rs0"])
-    iota("i6", T.m2[:], [[0, 17], [8, 2]], -6, 0, ["m2"])
-    zero("i7", T.f2[:, 0:258:257], 2, ["f2y"])
-    zero("i7", T.f2[:, 528:786:257], 2, ["f2z"])
-    iota("i7", T.alt[:], [[0, 136], [1, 2]], 0, 0, ["alt"])
-    zero("i7", T.yt[:, 264:512], 248, ["ytz"])
-    zero("i8", T.zt[:], 512, ["zt"])
-    zero("i8", T.ht[:, 264:512], 248, ["htz"])
-    zero("i8", T.dtb[:], 192, ["d1", "d2", "d3"])
-    iota("i8", T.nt[:], [[0, 3], [1, 64]], 0, 0, ["nt"])
+    zero("i6", T.lt[:, 4 * 656:4 * 704], 192, ["z2"])
+    zero("i7", T.lt[:, 4 * 464:4 * 512], 192, ["z3"])
+    zero("i8", T.lt[:, 4 * 208:4 * 256], 192, ["z0"])
+    zero("i9", T.lt[:, 4 * 400:4 * 448], 192, ["z1"])
+    zero("i10", T.lt[:, 4 * 512:4 * 576], 256, ["z4"])
+    zero("i11", T.rs[:, 0:1], 1, ["rs0"])
+    iota("i12", T.a16w[:], [[0, 18], [1, 16]], 0, 0, ["a16w"])
+    op("v", "k0", lambda: V.memset(T.eb[:], 0.0), (), ["eb"])
+    for j, m in enumerate([15, 8, 4, 2, 1]):
+        ts("k1", col(T.ci, j), col(T.pi, j), m, None, A.bitwise_and, None, ["pi"], ["ci%d" % j])
+    ts("k3", T.eb[:, 3:515:4], T.d128[:], 0.0, None, A.is_equal, None, ["d128"], ["eb"])
+    cp("k5", T.cf[:, 0:5], T.ci[:, 0:5], ["ci%d" % j for j in range(5)], ["cf"])
+    for b in range(4):
+        quant("k6", *side(T.qe, T.se, b), T.eb[:, 3 - b:515 - b], ["eb"], ["qe%d" % b])
+    ts("k8", T.lpk[:, 0:24], T.lpi[:], 0.125, None, A.mult, None, ["lpi"], ["lpk0", "lpk2", "lpk3"])
+    ts("k8", T.lpk[:, 24:32], T.lpi[:, 8:16], col(T.cf, PAR8), 0.125, A.add, A.mult, ["lpi", "cf"], ["lpk1"])
+    ts("k10", T.own[:], T.a16[:], col(T.cf, R), -BIG, A.not_equal, A.mult, ["a16", "cf"], ["own"])
+    ts("k10", T.d0g[:], T.a16[:], 0.0, -2 * BIG, A.is_equal, A.mult, ["a16"], ["d0g"])
+    quant("k12", T.qu[:], T.su[:], T.ut[:], ["ut"], ["qu"])
+    column("k17", 2, COL4, 0.5, -1.0)
+    column("k17", 3, COL4, -0.5 * TINY, TINY)
+    column("k17", 1, PAIR2, 128.5, 0.0)
+    column("k17", 5, R, -511.0, 7665.0)
+    column("k17", 0, LAST, -4096.0, 2048.0)
+    act("k18", T.d0d[:], T.a16[:], F.Sign, ["a16"], ["d0d"])
+    act("k4", T.gv[:], T.gv[:], F.Abs, ["gv"], ["gv"], bias=7.5)
+    act("k21", T.kt[:], T.a16[:, 0:16], F.Identity, ["a16", "cd5"], ["kt"], scale=-16.0, bias=col(T.cd, 5))
+    act("k11", T.gv[:], T.gv[:], F.Relu, ["gv"], ["gv"], scale=-1.0, bias=8.0)
+    act("k19", T.d0p[:], T.own[:], F.Identity, ["own"], ["d0p"], scale=-66048.0 / BIG, bias=-65536.0)
+    pick_scales("k14", 0)
+    pick_scales("k15", 1)
+    act("k20", T.jt[:], T.jr[:], F.Identity, ["jr", "cd1"], ["jt"], bias=col(T.cd, 1))
+    for j in range(4):
+        act("k7", T.wab[:, j:512:4], T.gv[:], F.Sign, ["gv"], ["wab%d" % j])
+    iota("i13", T.m2[:], [[0, 17], [8, 2]], -6, 0, ["m2"])
+    zero("i14", T.f2[:, 0:258:257], 2, ["f2y"])
+    zero("i14", T.f2[:, 528:786:257], 2, ["f2z"])
+    iota("i14", T.alt[:], [[0, 136], [1, 2]], 0, 0, ["alt"])
+    zero("i14", T.yt[:, 264:512], 248, ["ytz"])
+
+    def late_constants():
+        iota("i15", T.a4[:], [[0, 32], [4, 4]], 0, 0, ["a4"])
+        zero("i16", T.ht[:, 264:512], 248, ["htz"])
+        for j, (pat, base) in enumerate([([[1, 4], [8, 34]], 0), ([[1, 4], [8, 34]], 4),
+                                         ([[1, 4], [16, 17], [12, 2]], 0), ([[1, 4], [16, 17], [4, 2]], 4)]):
+            iota("i17", part(T.tb, j, 136), pat, base, 0, ["tb%d" % j])
+        for j, (pat, base) in enumerate([([[2, 16], [-135, 2], [0, 2]], 408), ([[1, 32], [136, 2]], 0), ([[2, 16], [137, 2], [0, 2]], 272)]):
+            iota("i18", part(T.ptab, j, 64), pat, base, 0, ["ptab%d" % j])
+
+    def later_constants():
+        zero("i19", T.dtb[:], 192, ["d1", "d2", "d3"])
+        iota("i19", T.nt[:], [[0, 3], [1, 64]], 0, 0, ["nt"])
+        for j in range(3):
+            iota("i20", part(T.ndt, j), [[1, 64], [j + 1, 2]], 0, 0, ["ndt%d" % j])
+        iota("i21", T.ndt[:, 127:254:126], [[0, 2]], 0, 0, ["ndt0", "ndt1"])
+        iota("i22", T.ndt[:, 255:382:126], [[0, 2]], 1, 0, ["ndt1", "ndt2"])
 
     slot = {t: ((16 - t) // 4, (16 - t) % 4) for t in range(1, 16)}
 
@@ -209,7 +240,7 @@ def rank_program(g, core, T, topo):
         return T.lt[:, 4 * TILES[j][0] + e:4 * TILES[j][0] + 64 * t:4]
 
     def lkeys(j):
-        return ["l%d" % t for t in slot if slot[t][0] == j] + (["l0"] if j == 0 else [])
+        return ["l%d" % t for t in slot if slot[t][0] == j] + (["dg0", "dg1"] if j == 0 else [])
 
     def wf(j, m=1):
         return T.wf[:, 16 * j:16 * (j + m)]
@@ -217,107 +248,160 @@ def rank_program(g, core, T, topo):
     def wi(j):
         return T.wi[:, 16 * j:16 * j + 16]
 
-    def cmp(*blocks):
+    def own_score(t):
+        return col(T.sg, 16 * t + 15)
+
+    def cmp(b, *blocks):
         for t in blocks:
-            ts("c%d_" % blocks[0], lview(t), bank(0, 0, 16 * t), col(T.sg, 16 * t + 15), None, A.is_lt, None,
-               ["#0", "sg", "z%d" % slot[t][0]], ["l%d" % t])
+            ts("c%d" % t, lview(t), bank(b, 0, 16 * t), own_score(t), None, A.is_lt, None,
+               ["#%d" % b, "sg%d" % (t // 8), "z%d" % slot[t][0]], ["l%d" % t])
+
+    def rows(*blocks):
         for t in blocks:
             act("rs", T.jk[:, 8 * t * (t - 1):8 * t * (t + 1)], lview(t), F.Identity, ["l%d" % t], ["rs%d" % t, "jk%d" % t],
-                scale=-1.0, bias=1.0, accum_out=col(T.rs, t))
+                accum_out=col(T.rs, t))
+
+    def cmp_rows(*blocks):
+        signs = {t: T.sgn[:, 8 * t * (t - 1):8 * t * (t + 1)] for t in blocks}
+        for t in blocks:
+            act("sn%d" % t, signs[t], bank(1, 0, 16 * t), F.Sign, ["#1", "sg%d" % (t // 8)], ["sn%d" % t], scale=-1.0, bias=own_score(t))
+        for t in blocks:
+            act("rl%d" % (t // 8), lview(t), signs[t], F.Relu, ["sn%d" % t, "z%d" % slot[t][0]], ["l%d" % t, "rs%d" % t],
+                accum_out=col(T.rs, t))
 
     def pack(tag, c, e, keys):
         quant(tag, T.ql[:, c:e], T.sl[:, c:e], T.lt[:, 4 * c:4 * e], keys, [tag])
 
-    def count(j, tag):
-        c, m = TILES[j]
-        mm("mp", bank(3, 0, m), *side(T.qa, T.sa, min(j, 1)), T.ql[:, c:c + m], T.sl[:, c:c + m], [tag, "qa"], ["#3"],
-           start=j == 0, stop=j == 2)
+    def count(tag, b, c, m, key, start=False, stop=False):
+        mm(tag, bank(b, 0, m), T.qa[:], T.sa[:], T.ql[:, c:c + m], T.sl[:, c:c + m], [key, "qa"], ["#%d" % b], start=start, stop=stop)
+
+    def offsets(h):
+        scan("xv%d" % h, part(T.xv, h), part(T.jt, h), part(T.tc, h), A.max, A.mult, ["jt", "tc%d" % h], ["xv%d" % h])
+
+    def scores(h, b):
+        tt("sm%d" % h, part(T.sm, h), bank(b, 128 * h, 128 * h + 128), T.own[:], A.add, ["#%d" % b, "own"], ["sm%d" % h])
+
+    def diagonal(h, b):
+        tt("dg%d" % h, T.lt[:, 512 * h:512 * h + 512:4], bank(b, 128 * h, 128 * h + 128), part(T.sg, h), A.is_le,
+           ["#%d" % b, "sg%d" % h] + ["z0"] * h, ["dg%d" % h])
+
+    def diagonal_rows(h):
+        scan("ds%d" % h, part(T.ds, h), T.d0d[:], T.lt[:, 512 * h:512 * h + 512:4], A.mult, A.add, ["d0d", "dg%d" % h], ["ds%d" % h])
 
     qx, sx = T.qx[:], T.sx[:]
+    QX = ["qx0", "qx1"]
     rid, pid = topo.addr(nxt)[:2]
 
     def colours():
         for j in range(2):
-            mm("me%d" % j, bank(j), *side(T.qp, T.sp, 2 + j), qx, sx, ["qx", "pc16", "ps16"], ["#%d" % j])
-            act("eo", T.eo[:, 256 * j:256 * j + 256], bank(j), F.Sign, ["#%d" % j], ["eo%d" % j])
+            mm("me%d" % j, bank(j), *side(T.qp, T.sp, 2 + j), qx, sx, QX + ["pc%d" % (2 + j), "ps%d" % (2 + j)], ["#%d" % j])
+            act("eo%d" % j, part(T.eo, j, 256), bank(j), F.Sign, ["#%d" % j], ["eo%d" % j], bias=-TINY)
+
+    def held_colours(*parts):
+        for h in parts:
+            hold("eh", T.eh, T.d0b, T.eo, h, ["d0b", "eo%d" % (h // 2)], ["eh%d" % h])
+
+    def served_colour(h):
+        mm("m2", bank(2, 0, 128), *side(T.qp, T.sp, 1), *side(T.qx, T.sx, h), ["qx%d" % h, "pc1", "ps1"], ["#2"])
+        act("cs%d" % h, part(T.tc, h), bank(2, 0, 128), F.Sign, ["#2", "cd2", "cd3"], ["tc%d" % h], scale=col(T.cd, 2), bias=col(T.cd, 3))
+
+    def first_half():
+        mm("ma", bank(3, 0, 128), *side(T.qp, T.sp, 0), *side(T.qx, T.sx, 0), ["qx0", "pc0", "ps0"], ["#3"])
+        served_colour(0)
+        mm("mb", bank(1, 0, 128), *side(T.qp, T.sp, 0), *side(T.qx, T.sx, 0), ["qx0"], ["#1"])
 
     for k in range(ROUNDS):
         first, last = k == 0, k == ROUNDS - 1
         if first:
-            quant("qx", qx, sx, T.xin[:], ["xin"], ["qx"])
-        mm("m0", bank(0), *side(T.qp, T.sp, 0), qx, sx, ["qx", "pc0", "ps0"], ["#0"])
-        if first:
-            pick_codes("k16", 8, 16)
-            pick_scales("k18", 8, 16)
-            pick_codes("k23", 16, 32)
-        mm("m2", bank(2), *side(T.qp, T.sp, 1), qx, sx, ["qx", "pc8", "ps8"], ["#2"])
+            quant("qx0", *side(T.qx, T.sx, 0), part(T.xin, 0, 512), ["xin0"], ["qx0"])
+            pick_codes("k13", 0)
+            quant("qx1", *side(T.qx, T.sx, 1), part(T.xin, 1, 512), ["xin1"], ["qx1"])
+            pick_codes("k22", 1)
+            first_half()
+            scores(0, 3)
+        mm("m0", bank(0), *side(T.qp, T.sp, 0), qx, sx, QX + ["pc0", "ps0"], ["#0"])
+        hold("sg0", T.sg, T.d0g, T.sm, 0, ["d0g", "sm0"], ["sg0"])
+        cmp_rows(7, 6)
+        served_colour(1)
+        mm("m1", bank(1), *side(T.qp, T.sp, 0), qx, sx, QX, ["#1"])
         for b in range(4):
-            mm("mf", bank(4 + b), *side(T.qe, T.se, b), qx, sx, ["qx", "qe%d" % b], ["#%d" % (4 + b)])
+            mm("mf", bank(4 + b), *side(T.qe, T.se, b), qx, sx, QX + ["qe%d" % b], ["#%d" % (4 + b)])
+        if not first:
+            offsets(0)
+        diagonal(0, 3)
+        cmp(3, 5)
+        scores(1, 0)
+        cmp(0, 4, 3)
+        hold("sg1", T.sg, T.d0g, T.sm, 1, ["d0g", "sm1"], ["sg1"])
+        rows(5, 4)
+        cmp(0, 2, 1)
+        cmp_rows(12, 10, 9)
+        cmp(0, 15, 14, 13)
+        diagonal(1, 0)
+        cmp(0, 11, 8)
+        rows(3, 2, 1, 15, 14, 13, 11, 8)
         if first:
-            for j in range(2, 8):
-                equal("k11", T.wab[:, 512 * (j // 4) + j % 4:512 * (j // 4) + 512:4], T.bm[:], ["bm"], ["wab%d" % j])
-            equal("k25", T.d0d[:], T.mask[:], ["mask"], ["d0d"])
-        tt("sm", T.sm[:], bank(0), T.mask[:], A.mult, ["#0", "mask"], ["sm"])
-        scan("sg", T.sg[:], T.d0g[:], T.sm[:], A.mult, A.add, ["d0g", "sm"], ["sg"])
-        act("c1", T.tc[:], bank(2), F.Sign, ["#2"], ["tc"])
-        if first:
-            act("k19", T.d0p[:], T.mask[:], F.Identity, ["mask"], ["d0p"], scale=-66048.0, bias=512.0)
-            act("k26", T.jt[:], T.jr[:], F.Identity, ["jr", "cd1"], ["jt"], bias=col(T.cd, 1))
-        act("c2", T.rc[:], T.tc[:], F.Relu, ["tc", "cd2", "cd3"], ["rc"], scale=col(T.cd, 2), bias=col(T.cd, 3))
-        cmp(15)
-        cmp(14, 13)
-        cmp(12, 11)
-        tt("dg", T.lt[:, 0:1024:4], bank(0), T.sg[:], A.is_le, ["#0", "sg", "z0"], ["l0"])
-        cmp(10, 9)
-        if first:
-            quant("k17", T.qa[:], T.sa[:], T.wab[:], ["wab%d" % j for j in range(8)], ["qa"])
+            quant("k16", T.qa[:], T.sa[:], T.wab[:], ["wab%d" % j for j in range(4)], ["qa"])
         pack("qla", 0, 256, lkeys(0))
-        count(0, "qla")
-        cmp(4, 3, 2, 1)
-        scan("ds", T.ds[:], T.d0d[:], T.lt[:, 0:1024:4], A.mult, A.add, ["d0d", "l0"], ["ds"])
-        pack("qlb", 256, 576 if first else 512, lkeys(1) + lkeys(3))
-        count(1, "qlb")
-        count(3, "qlb")
-        cmp(8, 7)
-        cmp(6, 5)
-        ts("dc", T.pre[:, 0:16], T.ds[:, 15:256:16], col(T.cd, 5), None, A.add, None, ["ds", "cd5"], ["dc"])
+        count("mh", 2, 64, 192, "qla", start=True)
+        count("ml", 3, 0, 128, "qla", start=True)
+        pack("qlb", 256, 576 if first else 512, lkeys(1) + lkeys(3) + ["z4"])
+        count("mh", 2, 256 + 64, 128, "qlb", stop=True)
+        count("ml", 3, 256, 128, "qlb")
+        count("ml", 3, 448, 128, "qlb")
         pack("qlc", 576, 704, lkeys(2))
-        count(2, "qlc")
-        scan("xv", T.xv[:], T.jt[:], T.rc[:], A.max, A.min, ["jt", "rc"], ["xv"])
+        count("ml", 3, 576, 128, "qlc", stop=True)
+        diagonal_rows(0)
+        diagonal_rows(1)
         if first:
-            ts("k21", T.msel[:], T.m2[:], col(T.cf, 2), 2.0 ** 21, A.subtract, A.mult, ["m2", "cf"], ["msel"])
-            equal("k22", T.d0r[:], T.d0r[:], ["d0r"], ["d0r"])
-            act("k24", T.d0s[:], T.d0r[:], F.Identity, ["d0r", "cd0"], ["d0s"], scale=-2.0 ** 25, bias=col(T.cd, 0))
-        scan("hp", T.hp[:], T.d0p[:], bank(3), A.add, A.max, ["d0p", "#3"], ["hp"])
-        tt("pre", T.pre[:, 16:32], T.rs[:], T.pre[:, 0:16], A.subtract, ["dc"] + ["rs%d" % t for t in range(16)], ["pre"])
-        tt("lp", T.lp[:], T.hp[:, 15:256:16], T.pre[:, 16:32], A.add, ["hp", "pre"], ["lp"])
+            offsets(0)
+            ts("k23", T.msel[:], T.m2[:], col(T.cf, PAR8), 2.0 ** 21, A.subtract, A.mult, ["m2", "cf"], ["msel"])
+            column("k24", 4, PAR8, -2.0 ** 19, 2.0 ** 22)
+        scan("hp1", part(T.hp, 1), T.d0p[:], bank(2, 64, 192), A.add, A.max, ["d0p", "#2"], ["hp1"])
+        tt("dc", T.pre[:, 0:16], T.ds[:, 15:256:16], T.kt[:], A.add, ["ds0", "ds1", "kt"], ["dc"])
+        scan("hp0", part(T.hp, 0), T.d0p[:], bank(3, 0, 128), A.add, A.max, ["d0p", "#3"], ["hp0"])
+        tt("pre", T.pre[:, 16:32], T.rs[:], T.pre[:, 0:16], A.add, ["dc"] + ["rs%d" % t for t in range(16)], ["pre"])
+        offsets(1)
+        tt("lp", T.lp[:], T.hp[:, 15:256:16], T.pre[:, 16:32], A.subtract, ["hp0", "hp1", "pre"], ["lp"])
+        if first:
+            act("k26", T.d0s[:], T.a16w[:, 0:280], F.Abs, ["a16w", "cf"], ["d0s"], scale=-1.0, bias=col(T.cf, PAR8))
+            act("k27", col(T.d0s, 256), col(T.a16w, 0), F.Identity, ["d0s"], ["d0s"])
+            act("k28", T.d0s[:], T.d0s[:], F.Relu, ["d0s"], ["d0s"], scale=-1.0, bias=1.0)
+            act("k29", T.d0s[:], T.d0s[:], F.Identity, ["d0s", "cd0"], ["d0s"], scale=-2.0 ** 25, bias=col(T.cd, 0))
+            ts("k30", col(T.msel, 31), col(T.cd, 0), col(T.cf, PAR8), col(T.cd, 4), A.mult, A.add, ["cd0", "cd4", "msel"], ["msel"])
+            column("k31", 6, R, 2.0, 34.5)
         for b in (0, 2, 1, 3):
             o = 528 * (b % 2) + 1 + 257 * (b // 2)
             act("f%d" % (b % 2), T.f2[:, o:o + 256], bank(4 + b), F.Copy, ["#%d" % (4 + b)], ["f%d" % b])
         if not first:
             colours()
-        cp("xo", T.xo[:, 0:256].indirect(T.lp[:]), T.xv[:], ["lp", "xv"], ["xo"])
+        cp("xo", T.xo[:, 0:256].indirect(T.lp[:]), T.xv[:], ["lp", "xv0", "xv1"], ["xo"])
         ts("w0", wi(0), T.lp[:], 248.0, None, A.add, None, ["lp"], ["w0"])
-        cp("xw", T.xo[:, 256:280], T.xo[:, 0:24], ["xo"], ["xw"])
+        scan("na", T.na[:, 256:280], T.d0s[:, 256:280], T.xo[:, 0:24], A.add, A.max, ["d0s", "xo"], ["nb"])
+        scan("na", T.na[:, 0:256], T.d0s[:, 0:256], T.xo[:], A.add, A.max, ["d0s", "xo"], ["na"])
         ts("w1", wi(1), wi(0), 2, 62, A.logical_shift_right, A.bitwise_and, ["w0"], ["w1"])
-        scan("na", T.na[:], T.d0s[:], T.xo[:, 0:280], A.add, A.max, ["d0s", "xo", "xw"], ["na"])
+        scan("s1", T.s1[:], T.msel[:], T.na[:, 15:280:8], A.add, A.max, ["na", "nb", "msel"], ["s1"])
         ts("w2", wi(2), wi(0), 3, 1, A.logical_shift_right, A.bitwise_and, ["w0"], ["w2"])
-        scan("s1", T.s1[:], T.msel[:], T.na[:, 15:280:8], A.add, A.max, ["na", "msel"], ["s1"])
-        ts("w3", wf(0), wi(2), -2.0, 1.0, A.mult, A.add, ["w2"], ["sgn"])
         ts("s2", T.s2[:, 0:17], T.s1[:, 1:34:2], 1.5 * 2.0 ** 34, 1.5 * 2.0 ** 34, A.add, A.subtract, ["s1"], ["s2"])
+        ts("w3", wf(0), wi(1), col(T.cd, 6), None, A.add, None, ["w1", "cd6"], ["base"])
         tt("l1", T.l1[:, 0:17], T.s1[:, 1:34:2], T.s2[:, 0:17], A.subtract, ["s1", "s2"], ["l1"])
+        ts("w4", wf(1), wi(2), 63.5, -31.5, A.mult, A.add, ["w2"], ["ce"])
         act("g1", T.gz[:, 272:544], T.f2[:, 528:1042].indirect(T.l1[:, 0:17]), F.Copy, ["l1", "f1", "f3", "f2z"], ["g1"], scale=0.25)
-        if first:
-            pick_scales("k27", 16, 32)
-            column(4, 0, -4.0, 60.0)
-            colours()
         ts("g0", T.gz[:, 0:272], T.f2[:, 0:514].indirect(T.l1[:, 0:17]), 0.25, None, A.mult, None, ["l1", "f0", "f2", "f2y"], ["g0"])
+        ts("w4", wf(2), wi(2), -63.5, 32.0, A.mult, A.add, ["w2"], ["co"])
+        if first:
+            late_constants()
+            pick_scales("k32", 2)
+            pick_scales("k33", 3)
+            act("k34", T.d0b[:], T.own[:], F.Identity, ["own"], ["d0b"], scale=-260.0 / BIG, bias=-256.0)
         for w in range(2):
             o = 272 * w
             scan("zz%d" % w, T.zz[:, o:o + 272], T.alt[:], T.gz[:, o:o + 272], A.mult, A.add, ["alt", "g%d" % w], ["zz%d" % w])
         for w in range(2):
             o = 272 * w
             tt("y", T.yt[:, w:264:2], T.zz[:, o + 1:o + 264:2], T.zz[:, o + 9:o + 272:2], A.add, ["zz%d" % w], ["y%d" % w])
+        if not first:
+            held_colours(0, 1)
         quant("qy", *side(T.qy, T.sy, k), T.yt[:], ["y0", "y1", "ytz"], ["qy%d" % k])
         a, c = LAND[k], 128 * k
         arr = T.sem["arr%d" % k]
@@ -326,76 +410,123 @@ def rank_program(g, core, T, topo):
         op("g", None, lambda a=a, c=c, arr=arr: g.remote_dma(
             T.ls[:, a:a + NY], T.sy[:, c:c + NY], arr, T.sem.sent, pid, rid, topo.mask(core, nxt)), [])
         if first:
-            quant("k28", T.lc[:, 208:336], T.ls[:, 208:336], T.zt[:], ["zt"], ["lz"])
-            for j in range(2):
-                ts("k29", T.d0b[:, 256 * j:256 * j + 256], T.mask[:], -260.0, 4.0, A.mult, A.add, ["mask"], ["d0b%d" % j])
-        scan("eh", T.eh[:], T.d0b[:], T.eo[:], A.add, A.max, ["d0b0", "d0b1", "eo0", "eo1"], ["eh"])
+            later_constants()
+            pick_codes("k35", 2)
+            pick_codes("k36", 3)
+            colours()
+            op("v", "k37", lambda: V.memset(T.zt[:], 0.0), (), ["zt"])
+            for h in range(4):
+                hold("k38", T.tbh, T.d0p, T.tb, h, ["tb%d" % j for j in range(4)], ["tbh%d" % h])
+            scan("k38", T.tbh[:, 512:544], T.d0p[:, 0:32], T.tb[:, 512:544], A.add, A.max, ["tb3"], ["tbh4"])
+            quant("k39", T.lc[:, 208:336], T.ls[:, 208:336], T.zt[:], ["zt"], ["lz"])
+            column("k40", 7, R, 512.0, -7680.0)
+            act("k40", col(T.cd, 8), col(T.cf, COL4), F.Identity, ["cf"], ["cd8"], bias=col(T.cf, PAR8))
+            column("k40", 10, R, 34.0, -1548.0)
+            column("k40", 14, R, 4.0, -60.0)
+            act("k44", col(T.cd, 13), col(T.cd, 8), F.Identity, ["cd8", "cd10"], ["cd13"], scale=95.0, bias=col(T.cd, 10))
+            act("k46", T.a4[:], T.a4[:], F.Abs, ["a4", "cd8"], ["a4"], scale=-1.0, bias=col(T.cd, 8))
+            act("k47", T.a4[:], T.a4[:], F.Sign, ["a4"], ["a4"])
+            act("k48", T.d0c[:], T.a4[:], F.Identity, ["a4"], ["d0c"], scale=260.0, bias=-256.0)
+            act("k48", T.d0l[:], T.a4[:], F.Identity, ["a4"], ["d0l"], scale=66048.0, bias=-65536.0)
+            ts("k49", T.lw[:], T.tbh[:, 15:544:16], col(T.cd, 7), None, A.add, None, ["cd7"] + ["tbh%d" % h for h in range(5)], ["lw"])
+            held_colours(0, 1)
+        held_colours(2, 3)
+        for b in range(4):
+            act("fi", T.fi[:, b:4 * NA:4], bank(4 + b, 0, NA), F.Copy, ["#%d" % (4 + b)], ["fi%d" % b])
+        tt("w5", wf(3, 2), T.eh[:, 15:512:16], wf(1, 2), A.mult, ["eh%d" % h for h in range(4)] + ["ce", "co"], ["w5"])
         if k == 1:
-            quant("k30", T.qv[:], T.sv[:], T.vt[:], ["vt"], ["qv"])
-        ts("w4", wf(1, 2), T.eh[:, 15:512:16], col(T.cd, 4), 0.0, A.subtract, A.is_gt, ["eh", "cd4"], ["e", "o"])
-        tt("w5", wf(3), wf(2), wf(1), A.subtract, ["e", "o"], ["dd"])
-        tt("w5", wf(4), wf(1), wi(1), A.add, ["e", "w1"], ["t1"])
-        tt("w6", wf(5), wf(3), wf(0), A.mult, ["dd", "sgn"], ["u"])
-        tt("w6", wf(6), wf(3), wi(2), A.mult, ["dd", "w2"], ["q"])
-        ts("w7", wf(8), wf(5), 64.0, 64.0, A.mult, A.add, ["u"], ["t2"])
-        tt("w7", wf(7), wf(4), wf(6), A.add, ["t1", "q"], ["m"])
-        ts("w8", wf(9), wf(5), 2.0, None, A.add, None, ["u"], ["dl"])
-        tt("w9", T.lcb[:], wf(8), wf(7), A.add, ["t2", "m"], ["lcb"])
+            quant("k50", T.qv[:], T.sv[:], T.vt[:], ["vt"], ["qv"])
+        tt("w6", wf(5), wf(3), wf(0), A.add, ["w5", "base"], ["w6"])
+        tt("w7", T.lcb[:], wf(5), wf(4), A.add, ["w5", "w6"], ["lcb"])
+        act("lob", T.lob[:], T.ptab[:, 0:192].indirect(T.lcb[:]), F.Copy, ["lcb", "ptab0", "ptab1", "ptab2"], ["lob"])
+        if last:
+            ts("w8", wf(6), T.lcb[:], 2.0, col(T.cd, 14), A.mult, A.add, ["lcb", "cd14"], ["lo16"])
         got = (arr, 2 * len(topo.engines(prv, core)))
         for b in range(4):
             mm("mr%d" % b, bank(b, 0, 128), *side(T.qw, T.sw, b), T.lc[:, a:a + 128], T.ls[:, a:a + 128], ["qw", "sw", "lz"], ["#%d" % b],
                ext=got if b == 0 else None)
-        ts("w10", wf(10), wf(9), col(T.cd, 4), None, A.mult, None, ["dl", "cd4"], ["cl"])
         for b in range(4):
             if b % 2 == 0:
                 act("ha", T.ht[:, b:264:4], bank(b, 0, NY), F.Copy, ["#%d" % b], ["h%d" % b], scale=0.03125)
             else:
                 ts("hv", T.ht[:, b:264:4], bank(b, 0, NY), 0.03125, None, A.mult, None, ["#%d" % b], ["h%d" % b])
         quant("qh", T.qh[:], T.sh[:], T.ht[:], ["h0", "h1", "h2", "h3", "htz"], ["qh"])
-        tt("w11", wf(11), wf(7), wf(10), A.subtract, ["m", "cl"], ["lo"])
-        act("th", T.th[:], T.nt[:, 0:192].indirect(T.lcb[:]), F.Relu, ["lcb", "nt"], ["th"], scale=2.0 ** -100, bias=-61.5 * 2.0 ** -100)
-        for b in range(4):
-            act("hq", T.hpl[:, 80 * b:80 * b + NY], T.ht[:, b:264:4], F.Copy, ["h%d" % b], ["hq%d" % b])
-        mm("mv", bank(4, 0, 128), *side(T.qp, T.sp, 0), T.qh[:], T.sh[:], ["qh"], ["#4"])
-        cp("vs", T.vs[:], bank(4, 0, NY), ["#4"], ["vs"])
-        tt("d", T.dtb[:, 1:64:2], T.vs[:, 1:64:2], bank(4, 2, 65, 2), A.subtract, ["#4", "vs"], ["d1"])
-        tt("d", T.dtb[:, 64:128], T.vs[:, 0:64], bank(4, 2, 66), A.subtract, ["#4", "vs"], ["d2"])
-        tt("d", T.dtb[:, 128:192:2], T.vs[:, 0:63:2], bank(4, 3, 66, 2), A.subtract, ["#4", "vs"], ["d3"])
-        tt("bt", T.bt[:], T.dtb[:, 0:192].indirect(T.lcb[:]), T.th[:], A.is_lt, ["d1", "d2", "d3", "lcb", "th"], ["bt"])
-        scan("bh", T.bh[:], T.d0b[:, 0:256], T.bt[:], A.add, A.max, ["bt"], ["bh"])
-        tt("fa", T.fa[:], T.bh[:, 15:256:16], wf(9), A.mult, ["bh", "dl"], ["fa"])
-        tt("lh", T.lh[:], T.fa[:], wf(11), A.add, ["fa", "lo"], ["lh"])
-        for b in (2, 3):
-            act("gh%d" % b, T.gh[:, 256 * (b - 2):256 * (b - 1)], T.hpl[:, 80 * b:80 * b + NY].indirect(T.lh[:]), F.Copy,
-                ["lh", "hq%d" % b], ["gh%d" % b])
-        for b in (0, 1):
-            tt("x", T.xs[:, b:1024:4], T.hpl[:, 80 * b:80 * b + NY].indirect(T.lh[:]), T.f2[:, 528 * b + 1:528 * b + 257], A.add,
-               ["lh", "hq%d" % b, "f%d" % b], ["x%d" % b])
-        for b in (2, 3):
-            tt("x", T.xs[:, b:1024:4], bank(4 + b), T.gh[:, 256 * (b - 2):256 * (b - 1)], A.add, ["#%d" % (4 + b), "gh%d" % b], ["x%d" % b])
+        act("th", T.th[:], T.nt[:, 0:192].indirect(T.lcb[:]), F.Relu, ["lcb", "nt"], ["th"], scale=TINY, bias=-61.5 * TINY)
+        act("hw", T.hw[:], T.ht[:, 0:272].indirect(T.lw[:]), F.Copy, ["h0", "h1", "h2", "h3", "htz", "lw"], ["hw"])
+        mm("mv", bank(0, 0, 128), *side(T.qp, T.sp, 0), T.qh[:], T.sh[:], ["qh"], ["#0"])
+        for h in range(2):
+            hold("l4", T.l4, T.d0l, T.lob, h, ["d0l", "lob"], ["l4%d" % h])
+        cp("vs", T.vs[:], bank(0, 0, NY), ["#0"], ["vs"])
+        ts("lo4", T.lo4[:], T.l4[:, 3:256:4], col(T.cd, 13), None, A.add, None, ["l40", "l41", "cd13"], ["lo4"])
+        tt("d", T.dtb[:, 1:64:2], T.vs[:, 1:64:2], bank(0, 2, 65, 2), A.subtract, ["#0", "vs"], ["d1"])
+        tt("d", T.dtb[:, 64:128], T.vs[:, 0:64], bank(0, 2, 66), A.subtract, ["#0", "vs"], ["d2"])
+        tt("d", T.dtb[:, 128:192:2], T.vs[:, 0:63:2], bank(0, 3, 66, 2), A.subtract, ["#0", "vs"], ["d3"])
+        for h in range(2):
+            tt("bt%d" % h, part(T.bt, h), T.dtb[:, 0:192].indirect(part(T.lcb, h, 8)), part(T.th, h), A.is_lt,
+               ["d1", "d2", "d3", "lcb", "th"], ["bt%d" % h])
+        for h in range(2):
+            hold("bh%d" % h, T.bh, T.d0c, T.bt, h, ["d0c", "bt%d" % h], ["bh%d" % h])
+        for h in range(2):
+            tt("lh%d" % h, part(T.lh, h, 32), T.bh[:, 128 * h + 3:128 * h + 128:4], part(T.lo4, h, 32), A.add, ["bh%d" % h, "lo4"], ["lh%d" % h])
+        for q in range(2):
+            act("gh%d" % q, part(T.gh, q, 256), T.hw[:, 0:544].indirect(part(T.lh, 2 + q, 16)), F.Copy, ["lh1", "hw"], ["gh%d" % q])
+        tt("xa", part(T.xs, 0, 512), T.hw[:, 0:544].indirect(part(T.lh, 0, 32)), T.fi[:], A.add,
+           ["lh0", "hw"] + ["fi%d" % b for b in range(4)], ["xa"])
+
+        def rest(*pieces):
+            for i in pieces:
+                q, b = divmod(i, 4)
+                tt("x", T.xs[:, 512 + 256 * q + b:768 + 256 * q:4], bank(4 + b, 128 + 64 * q, 192 + 64 * q), T.gh[:, 256 * q + b:256 * q + 256:4],
+                   A.add, ["#%d" % (4 + b), "gh%d" % q], ["x%d" % i])
+        rest(0, 1)
+        quant("qx0", *side(T.qx, T.sx, 0), part(T.xs, 0, 512), ["xa"], ["qx0"])
         if last:
-            act("nd", T.ndf[:], T.nt[:, 0:128].indirect(T.lh[:]), F.Copy, ["lh", "nt"], ["ndf"])
-            dma("s", "out", T.nd[:], T.ndf[0:128:16, :], ["ndf"], ["o0"])
-        quant("qx", qx, sx, T.xs[:], ["x0", "x1", "x2", "x3"], ["qx"])
+            mm("ma", bank(3, 0, 128), T.qv[:], T.sv[:], *side(T.qx, T.sx, 0), ["qx0", "qv"], ["#3"])
+        else:
+            first_half()
+        rest(2, 3, 4, 5, 6, 7)
+        if last:
+            for h in range(2):
+                hold("b16", T.b16, T.d0b, T.bt, h, ["bt%d" % h], ["b16%d" % h])
+        else:
+            scores(0, 3)
+        quant("qx1", *side(T.qx, T.sx, 1), part(T.xs, 1, 512), ["x%d" % b for b in range(8)], ["qx1"])
 
-    for j in range(2):
-        mm("m%d" % (2 * j), bank(2 * j, 0, 128), T.qv[:], T.sv[:], *side(T.qx, T.sx, j), ["qx", "qv"], ["#%d" % (2 * j)])
-    dma("s", "out", T.oc[:], T.qx[:].bitcast(dt.uint8), ["qx"], ["o1"])
+    tt("ln", T.ln[:], T.b16[:, 15:256:16], wf(6), A.add, ["b160", "b161", "lo16"], ["ln"])
+    mm("m1", bank(1, 0, 128), T.qv[:], T.sv[:], *side(T.qx, T.sx, 1), ["qx1", "qv"], ["#1"])
+    dma("s", "out", part(T.oc, 0, 512), part(T.qx, 0).bitcast(dt.uint8), ["qx0"], ["o1"])
+    act("cs0", part(T.yo, 0), bank(3, 0, 128), F.Copy, ["#3"], ["yo0"])
+    dma("a", "out", part(T.y, 0), part(T.yo, 0), ["yo0"], ["o2"])
+    act("nd", T.ndf[:], T.ndt[:, 0:384].indirect(T.ln[:]), F.Copy, ["ln", "ndt0", "ndt1", "ndt2"], ["ndf"])
+    dma("s", "out", part(T.oc, 1, 512), part(T.qx, 1).bitcast(dt.uint8), ["qx1"], ["o3"])
     for j in range(4):
-        dma("as"[j % 2], "out", T.osc[4 * j:4 * j + 4, :], T.sx[32 * j:32 * j + 4, :], ["qx"], ["o%d" % (2 + j)])
-    cp("yo", T.yo[:, 0:128], bank(0, 0, 128), ["#0"], ["yo0"])
-    dma("s", "out", T.y[:, 0:128], T.yo[:, 0:128], ["yo0"], ["o6"])
-    act("c1", T.yo[:, 128:256], bank(2, 0, 128), F.Copy, ["#2"], ["yo1"])
-    dma("a", "out", T.y[:, 128:256], T.yo[:, 128:256], ["yo1"], ["o7"])
-    op("g", None, None, ["o%d" % j for j in range(8)], ext=(T.sem.sent, 2 * ROUNDS * len(topo.engines(core, nxt))))
+        dma("sa"[j // 3], "out", T.osc[4 * j:4 * j + 4, :], T.sx[32 * j:32 * j + 4, :], QX, ["o%d" % (4 + j)])
+    dma("a", "out", T.nd[:], T.ndf[0:128:16, :], ["ndf"], ["o0"])
+    cp("yo", part(T.yo, 1), bank(1, 0, 128), ["#1"], ["yo1"])
+    dma("s", "out", part(T.y, 1), part(T.yo, 1), ["yo1"], ["o8"])
+    op("g", None, None, ["o%d" % j for j in range(9)], ext=(T.sem.sent, 2 * ROUNDS * len(topo.engines(core, nxt))))
 
-    assert len(tags) <= NSEM
+    sems, place = [], {}
+    for tag, t in tags.items():
+        raised = t["ops"][:t["closed"]]
+        if not raised:
+            continue
+        bits, plain = sum(1 << o for o in raised), ops[raised[0]]["inc"] == 1
+        free = [s for s in sems if plain and s["plain"] and s["bits"] & ~ops[raised[0]]["know"] == 0]
+        if not free:
+            free = [{"name": "s%d" % len(sems), "bits": 0, "sum": 0, "plain": plain}]
+            sems.append(free[0])
+        place[tag] = (T.sem[free[0]["name"]], free[0]["sum"])
+        free[0]["bits"] |= bits
+        free[0]["sum"] += sum(ops[o]["inc"] for o in raised)
     for i, o in enumerate(ops):
-        for sem, val in o["waits"]:
-            queue[o["q"]].wait_ge(sem, val)
+        if o["ext"]:
+            queue[o["q"]].wait_ge(*o["ext"])
+        for tag, val in o["waits"]:
+            queue[o["q"]].wait_ge(place[tag][0], place[tag][1] + val)
         if o["fn"] is None:
             continue
         ins = o["fn"]()
         t = tags.get(o["tag"])
         if t and i in t["ops"][:t["closed"]]:
-            ins.then_inc(T.sem["s%d" % t["sem"]], o["inc"])
+            ins.then_inc(place[o["tag"]][0], o["inc"])

@@ -5,9 +5,9 @@ F = ActivationFunctionType
 C4, U8, BF, F32, I32, U16 = "float8_e4m3fn_x4", "uint8", "bfloat16", "float32", "int32", "uint16"
 ROUNDS = 3
 NY = 66
-NA = 128
 LAND = [142, 76, 10]
-TILES = [(0, 256), (256, 192), (576, 128), (448, 128)]
+TILES = [0, 256, 512, 640]
+STEP = 8192.0
 TINY, BIG = 2.0 ** -100, 2.0 ** 90
 
 
@@ -21,26 +21,26 @@ SCRATCH = {
     "qu": _s(128, C4), "su": _s(128, U8), "qp": _s(512, C4), "sp": _s(512, U8),
     "qv": _s(128, C4), "sv": _s(128, U8), "qw": _s(512, C4), "sw": _s(512, U8),
     "qx": _s(256, C4), "sx": _s(256, U8), "qe": _s(512, C4), "se": _s(512, U8),
-    "qa": _s(128, C4), "sa": _s(128, U8), "ql": _s(704, C4), "sl": _s(704, U8),
+    "qa": _s(128, C4), "sa": _s(128, U8), "ql": _s(768, C4), "sl": _s(768, U8),
     "qy": _s(384, C4), "sy": _s(384, U8), "lc": _s(336, C4), "ls": _s(336, U8),
     "qh": _s(128, C4), "sh": _s(128, U8),
     "pi": _s(8, I32), "ci": _s(8, I32), "cf": _s(8, F32), "cd": _s(16, F32), "lpi": _s(24, I32), "lpk": _s(32, U16),
     "a16": _s(128, F32), "a16w": _s(288, F32), "a4": _s(128, F32), "gv": _s(128, F32), "d128": _s(128, F32),
-    "jr": _s(256, F32), "jt": _s(256, F32), "kt": _s(16, F32),
-    "m2": _s(34, F32), "msel": _s(34, F32), "alt": _s(272, BF), "nt": _s(192, F32), "zt": _s(512, BF),
+    "jr": _s(256, F32), "jt": _s(256, F32), "kt": _s(16, F32), "flip": _s(64, F32),
+    "m2": _s(34, F32), "msel": _s(34, F32), "alt": _s(144, BF), "nt": _s(192, F32), "zt": _s(512, BF),
     "own": _s(128, F32), "d0g": _s(128, F32), "d0d": _s(128, BF), "d0p": _s(128, F32), "d0b": _s(128, BF),
     "d0c": _s(128, BF), "d0l": _s(128, F32), "d0s": _s(280, F32), "eb": _s(520, BF), "wab": _s(512, BF),
     "tb": _s(544, F32), "tbh": _s(544, F32), "lw": _s(34, U16), "ptab": _s(192, F32), "ndt": _s(384, F32),
     "sm": _s(256, F32), "sg": _s(256, F32), "tc": _s(256, BF), "sgn": _s(1920, BF),
-    "lt": _s(2816, BF), "jk": _s(1920, BF), "rs": _s(16, F32),
+    "lt": _s(3072, BF), "jk": _s(1920, BF), "rs": _s(16, F32),
     "ds": _s(256, BF), "pre": _s(32, F32), "hp": _s(256, F32), "lp": _s(16, U16),
-    "xv": _s(256, F32), "xo": _s(256, F32), "na": _s(280, F32), "s1": _s(34, F32), "s2": _s(18, F32),
-    "l1": _s(18, U16), "f2": _s(1056, BF), "fi": _s(4 * NA, BF), "gz": _s(544, BF), "zz": _s(544, BF),
+    "xv": _s(256, F32), "xo": _s(256, F32), "na": _s(280, F32), "s1": _s(34, F32), "s2": _s(34, BF),
+    "l1": _s(18, U16), "f2": _s(1056, BF), "fi": _s(640, BF), "gz": _s(576, BF), "zz": _s(576, BF),
     "yt": _s(512, BF), "eo": _s(512, BF), "eh": _s(512, BF), "wi": _s(48, I32), "wf": _s(128, F32),
     "lcb": _s(16, U16), "th": _s(256, F32), "lob": _s(256, F32), "l4": _s(256, F32), "lo4": _s(64, F32),
     "ht": _s(512, BF), "hw": _s(544, BF), "vs": _s(66, F32),
     "dtb": _s(192, F32), "bt": _s(256, BF), "bh": _s(256, BF), "b16": _s(256, BF), "lh": _s(64, U16), "ln": _s(16, U16),
-    "gh": _s(1024 - 4 * NA, BF), "ndf": _s(256, F32), "yo": _s(256, F32),
+    "gh": _s(512, BF), "ndf": _s(256, F32), "yo": _s(256, F32),
 }
 NSEM = 140
 SEMAPHORES = ["s%d" % i for i in range(NSEM)] + ["sent", "arr0", "arr1", "arr2"]
@@ -146,12 +146,12 @@ def rank_program(g, core, T, topo):
     def pick_list(b):
         return part(T.lpk, [0, 3, 1, 2][b], 8)
 
-    def pick_codes(tag, b):
-        cp(tag, part(T.qp, b).bitcast(dt.uint32), T.qu[:, 0:128].bitcast(dt.uint32).indirect(pick_list(b)),
+    def pick_codes(b):
+        cp("pc%d" % b, part(T.qp, b).bitcast(dt.uint32), T.qu[:, 0:128].bitcast(dt.uint32).indirect(pick_list(b)),
            ["qu", "lpk%d" % b], ["pc%d" % b])
 
-    def pick_scales(tag, b):
-        act(tag, part(T.sp, b), T.su[:, 0:128].indirect(pick_list(b)), F.Copy, ["qu", "lpk%d" % b], ["ps%d" % b])
+    def pick_scales(b):
+        act("ps%d" % b, part(T.sp, b), T.su[:, 0:128].indirect(pick_list(b)), F.Copy, ["qu", "lpk%d" % b], ["ps%d" % b])
 
     def column(tag, j, src, sc, bi):
         if isinstance(bi, int):
@@ -162,85 +162,87 @@ def rank_program(g, core, T, topo):
     def hold(tag, out, d0, a, h, r, w):
         scan(tag, part(out, h), d0[:], part(a, h), A.add, A.max, r, w)
 
+    def unit(b):
+        quant("qe%d" % b, *side(T.qe, T.se, b), T.eb[:, 3 - b:515 - b], ["eb"], ["qe%d" % b])
+
+    def blank(tag, out, m, w):
+        act(tag, out, T.eb[:, 0:2 * m:2], F.Copy, ["eb0"], w)
+
     dma("a", "ldu", T.ut[:], T.u[:], [], ["ut"])
-    for h in range(2):
+    for h in (1, 0):
         dma("s", "ldx%d" % h, part(T.xin, h, 512), part(T.x, h, 512), [], ["xin%d" % h])
-    dma("s", "ldw", T.qw[:].bitcast(dt.uint8), T.wc[:], [], ["qw"])
+    dma("s", "ldw", T.qw[:].bitcast(dt.uint8), T.wc[:], ["xin0", "xin1"], ["qw"])
     dma("s", "ldw", T.sw[:], T.ws[:], [], ["sw"])
     dma("s", "ldv", T.vt[:], T.v[:], [], ["vt"])
 
     R, PAR8, COL4, PAIR2, LAST = range(5)
     iota("i0", T.pi[:], [[0, 8]], 0, 1, ["pi"], False)
     iota("i1", T.d128[:], [[1, 128]], 0, -1, ["d128"])
-    iota("i3", T.lpi[:], [[8, 3], [128, 8]], 0, 0, ["lpi"], False)
-    iota("i4", T.a16[:], [[0, 8], [1, 16]], 0, 0, ["a16"])
-    iota("i2", T.gv[:], [[16, 8], [0, 16]], 0, -1, ["gv"])
-    iota("i5", T.jr[:], [[1, 256]], 2 ** 20 + 1, 0, ["jr"])
-    zero("i6", T.lt[:, 4 * 656:4 * 704], 192, ["z2"])
-    zero("i7", T.lt[:, 4 * 464:4 * 512], 192, ["z3"])
-    zero("i8", T.lt[:, 4 * 208:4 * 256], 192, ["z0"])
-    zero("i9", T.lt[:, 4 * 400:4 * 448], 192, ["z1"])
-    zero("i10", T.lt[:, 4 * 512:4 * 576], 256, ["z4"])
-    zero("i11", T.rs[:, 0:1], 1, ["rs0"])
-    iota("i12", T.a16w[:], [[0, 18], [1, 16]], 0, 0, ["a16w"])
-    op("v", "k0", lambda: V.memset(T.eb[:], 0.0), (), ["eb"])
+    iota("i2", T.lpi[:], [[8, 3], [128, 8]], 0, 0, ["lpi"], False)
+    iota("i3", T.a16[:], [[0, 8], [1, 16]], 0, 0, ["a16"])
+    iota("i4", T.gv[:], [[16, 8], [0, 16]], 0, -1, ["gv"])
+    iota("i5", T.jr[:], [[1, 256]], 16 * int(STEP) + 1, 0, ["jr"])
+    zero("z3", T.lt[:, 4 * 656:4 * 704], 192, ["z3"])
+    zero("z4", T.lt[:, 4 * 704:4 * 768], 256, ["z4"])
+    zero("z5", T.lt[:, 4 * 448:4 * 512], 256, ["z5"])
+    zero("i6", T.rs[:, 0:1], 1, ["rs0"])
+    iota("i6", T.m2[:], [[0, 17], [8, 2]], -6, 0, ["m2"])
+    iota("i7", T.a16w[:], [[0, 18], [1, 16]], 0, 0, ["a16w"])
+    for j, (pat, base) in enumerate([([[1, 4], [8, 34]], 0), ([[1, 4], [8, 34]], 4),
+                                     ([[1, 4], [16, 17], [12, 2]], 0), ([[1, 4], [16, 17], [4, 2]], 4)]):
+        iota("i8", part(T.tb, j, 136), pat, base, 0, ["tb%d" % j])
+    iota("i9", T.a4[:], [[0, 32], [4, 4]], 0, 0, ["a4"])
+    zero("i10", T.f2[:, 0:258:257], 2, ["f2y"])
+    zero("i10", T.f2[:, 528:786:257], 2, ["f2z"])
+    zero("i10", T.yt[:, 264:512], 248, ["ytz"])
+    iota("i10", T.alt[:], [[0, 72], [1, 2]], 0, 0, ["alt"])
+    for j, (pat, base) in enumerate([([[2, 16], [-135, 2], [0, 2]], 408), ([[1, 32], [136, 2]], 0), ([[2, 16], [137, 2], [0, 2]], 272)]):
+        iota("i11", part(T.ptab, j, 64), pat, base, 0, ["ptab%d" % j])
+    iota("i12", T.flip[:], [[0, 32], [-1, 2]], 0, 0, ["flip"])
+    zero("i12", T.dtb[:, 128:192], 64, ["d3"])
+    iota("i12", T.nt[:], [[0, 3], [1, 64]], 0, 0, ["nt"])
+
+    op("v", "k0", lambda: V.memset(T.eb[:], 0.0), (), ["eb", "eb0"])
     for j, m in enumerate([15, 8, 4, 2, 1]):
         ts("k1", col(T.ci, j), col(T.pi, j), m, None, A.bitwise_and, None, ["pi"], ["ci%d" % j])
-    ts("k3", T.eb[:, 3:515:4], T.d128[:], 0.0, None, A.is_equal, None, ["d128"], ["eb"])
-    cp("k5", T.cf[:, 0:5], T.ci[:, 0:5], ["ci%d" % j for j in range(5)], ["cf"])
-    for b in range(4):
-        quant("k6", *side(T.qe, T.se, b), T.eb[:, 3 - b:515 - b], ["eb"], ["qe%d" % b])
-    ts("k8", T.lpk[:, 0:24], T.lpi[:], 0.125, None, A.mult, None, ["lpi"], ["lpk0", "lpk2", "lpk3"])
-    ts("k8", T.lpk[:, 24:32], T.lpi[:, 8:16], col(T.cf, PAR8), 0.125, A.add, A.mult, ["lpi", "cf"], ["lpk1"])
-    ts("k10", T.own[:], T.a16[:], col(T.cf, R), -BIG, A.not_equal, A.mult, ["a16", "cf"], ["own"])
-    ts("k10", T.d0g[:], T.a16[:], 0.0, -2 * BIG, A.is_equal, A.mult, ["a16"], ["d0g"])
-    quant("k12", T.qu[:], T.su[:], T.ut[:], ["ut"], ["qu"])
-    column("k17", 2, COL4, 0.5, -1.0)
-    column("k17", 3, COL4, -0.5 * TINY, TINY)
-    column("k17", 1, PAIR2, 128.5, 0.0)
-    column("k17", 5, R, -511.0, 7665.0)
-    column("k17", 0, LAST, -4096.0, 2048.0)
-    act("k18", T.d0d[:], T.a16[:], F.Sign, ["a16"], ["d0d"])
-    act("k4", T.gv[:], T.gv[:], F.Abs, ["gv"], ["gv"], bias=7.5)
-    act("k21", T.kt[:], T.a16[:, 0:16], F.Identity, ["a16", "cd5"], ["kt"], scale=-16.0, bias=col(T.cd, 5))
-    act("k11", T.gv[:], T.gv[:], F.Relu, ["gv"], ["gv"], scale=-1.0, bias=8.0)
-    act("k19", T.d0p[:], T.own[:], F.Identity, ["own"], ["d0p"], scale=-66048.0 / BIG, bias=-65536.0)
-    pick_scales("k14", 0)
-    pick_scales("k15", 1)
-    act("k20", T.jt[:], T.jr[:], F.Identity, ["jr", "cd1"], ["jt"], bias=col(T.cd, 1))
+    ts("k2", T.eb[:, 3:515:4], T.d128[:], 0.0, None, A.is_equal, None, ["d128"], ["eb"])
+    cp("k3", T.cf[:, 0:5], T.ci[:, 0:5], ["ci%d" % j for j in range(5)], ["cf"])
+    for j, e in enumerate([256, 448, 640]):
+        blank("z%d" % j, T.lt[:, 4 * e - 192:4 * e], 192, ["z%d" % j])
+    ts("k4", T.lpk[:, 0:24], T.lpi[:], 0.125, None, A.mult, None, ["lpi"], ["lpk0", "lpk2", "lpk3"])
+    unit(0)
+    unit(1)
+    ts("k4", T.lpk[:, 24:32], T.lpi[:, 8:16], col(T.cf, PAR8), 0.125, A.add, A.mult, ["lpi", "cf"], ["lpk1"])
+    ts("k5", T.own[:], T.a16[:], col(T.cf, R), -BIG, A.not_equal, A.mult, ["a16", "cf"], ["own"])
+    unit(2)
+    quant("qu", T.qu[:], T.su[:], T.ut[:], ["ut"], ["qu"])
+    column("k7", 2, COL4, 0.5, -1.0)
+    column("k7", 3, COL4, -0.5 * TINY, TINY)
+    column("k7", 9, PAR8, 22.0 * STEP, 0.0)
+    column("k7", 5, R, -511.0, 7665.0)
+    act("k9", T.d0d[:], T.a16[:], F.Sign, ["a16"], ["d0d"])
+    column("k9", 1, PAIR2, 128.5, 9)
+    act("k9", T.kt[:], T.a16[:, 0:16], F.Identity, ["a16", "cd5"], ["kt"], scale=-16.0, bias=col(T.cd, 5))
+    act("k6", T.gv[:], T.gv[:], F.Abs, ["gv"], ["gv"], bias=7.5)
+    act("k6", T.d0g[:], T.d0d[:], F.Identity, ["d0d"], ["d0g"], scale=2 * BIG, bias=-2 * BIG)
+    pick_scales(0)
+    act("k8", T.gv[:], T.gv[:], F.Relu, ["gv"], ["gv"], scale=-1.0, bias=8.0)
+    pick_scales(1)
     for j in range(4):
-        act("k7", T.wab[:, j:512:4], T.gv[:], F.Sign, ["gv"], ["wab%d" % j])
-    iota("i13", T.m2[:], [[0, 17], [8, 2]], -6, 0, ["m2"])
-    zero("i14", T.f2[:, 0:258:257], 2, ["f2y"])
-    zero("i14", T.f2[:, 528:786:257], 2, ["f2z"])
-    iota("i14", T.alt[:], [[0, 136], [1, 2]], 0, 0, ["alt"])
-    zero("i14", T.yt[:, 264:512], 248, ["ytz"])
-
-    def late_constants():
-        iota("i15", T.a4[:], [[0, 32], [4, 4]], 0, 0, ["a4"])
-        zero("i16", T.ht[:, 264:512], 248, ["htz"])
-        for j, (pat, base) in enumerate([([[1, 4], [8, 34]], 0), ([[1, 4], [8, 34]], 4),
-                                         ([[1, 4], [16, 17], [12, 2]], 0), ([[1, 4], [16, 17], [4, 2]], 4)]):
-            iota("i17", part(T.tb, j, 136), pat, base, 0, ["tb%d" % j])
-        for j, (pat, base) in enumerate([([[2, 16], [-135, 2], [0, 2]], 408), ([[1, 32], [136, 2]], 0), ([[2, 16], [137, 2], [0, 2]], 272)]):
-            iota("i18", part(T.ptab, j, 64), pat, base, 0, ["ptab%d" % j])
-
-    def later_constants():
-        zero("i19", T.dtb[:], 192, ["d1", "d2", "d3"])
-        iota("i19", T.nt[:], [[0, 3], [1, 64]], 0, 0, ["nt"])
-        for j in range(3):
-            iota("i20", part(T.ndt, j), [[1, 64], [j + 1, 2]], 0, 0, ["ndt%d" % j])
-        iota("i21", T.ndt[:, 127:254:126], [[0, 2]], 0, 0, ["ndt0", "ndt1"])
-        iota("i22", T.ndt[:, 255:382:126], [[0, 2]], 1, 0, ["ndt1", "ndt2"])
+        act("k10", T.wab[:, j:512:4], T.gv[:], F.Sign, ["gv"], ["wab%d" % j])
+    act("k11", T.d0p[:], T.own[:], F.Identity, ["own"], ["d0p"], scale=-66048.0 / BIG, bias=-65536.0)
+    act("k11", T.jt[:], T.jr[:], F.Identity, ["jr", "cd1"], ["jt"], bias=col(T.cd, 1))
 
     slot = {t: ((16 - t) // 4, (16 - t) % 4) for t in range(1, 16)}
+    slot[8] = (0, 0)
+    within = [T.lt[:, 4 * TILES[2]:4 * TILES[2] + 512:4], T.lt[:, 512:1024:4]]
 
     def lview(t):
         j, e = slot[t]
-        return T.lt[:, 4 * TILES[j][0] + e:4 * TILES[j][0] + 64 * t:4]
+        return T.lt[:, 4 * TILES[j] + e:4 * TILES[j] + 64 * t:4]
 
     def lkeys(j):
-        return ["l%d" % t for t in slot if slot[t][0] == j] + (["dg0", "dg1"] if j == 0 else [])
+        return ["l%d" % t for t in slot if slot[t][0] == j] + {0: ["dg1"], 2: ["dg0"]}.get(j, [])
 
     def wf(j, m=1):
         return T.wf[:, 16 * j:16 * (j + m)]
@@ -275,18 +277,35 @@ def rank_program(g, core, T, topo):
     def count(tag, b, c, m, key, start=False, stop=False):
         mm(tag, bank(b, 0, m), T.qa[:], T.sa[:], T.ql[:, c:c + m], T.sl[:, c:c + m], [key, "qa"], ["#%d" % b], start=start, stop=stop)
 
+    def lower_counts(first):
+        pack("qlc", 512, 768 if first else 704, lkeys(2) + lkeys(3) + ["z4"])
+        count("ml", 3, 512, 128, "qlc", start=True)
+        count("ml", 3, 640, 128, "qlc")
+
+    def upper_counts(first):
+        pack("qlb", 256, 512 if first else 448, lkeys(1) + ["z5"])
+        count("mh", 2, 256 + 128, 128, "qlb", start=True)
+        count("ml", 3, 256, 128, "qlb")
+        pack("qld", 128, 256, lkeys(0))
+        count("mh", 2, 128, 128, "qld", stop=True)
+        pack("qla", 0, 128, lkeys(0))
+        count("ml", 3, 0, 128, "qla", stop=True)
+
     def offsets(h):
         scan("xv%d" % h, part(T.xv, h), part(T.jt, h), part(T.tc, h), A.max, A.mult, ["jt", "tc%d" % h], ["xv%d" % h])
 
-    def scores(h, b):
-        tt("sm%d" % h, part(T.sm, h), bank(b, 128 * h, 128 * h + 128), T.own[:], A.add, ["#%d" % b, "own"], ["sm%d" % h])
+    def scores(h):
+        tt("sm%d" % h, part(T.sm, h), bank(3 - h, 0, 128), T.own[:], A.add, ["#%d" % (3 - h), "own"], ["sm%d" % h])
+
+    def held_scores(h):
+        hold("sg%d" % h, T.sg, T.d0g, T.sm, h, ["d0g", "sm%d" % h], ["sg%d" % h])
 
     def diagonal(h, b):
-        tt("dg%d" % h, T.lt[:, 512 * h:512 * h + 512:4], bank(b, 128 * h, 128 * h + 128), part(T.sg, h), A.is_le,
-           ["#%d" % b, "sg%d" % h] + ["z0"] * h, ["dg%d" % h])
+        tt("dg%d" % h, within[h], bank(b, 128 * h, 128 * h + 128), part(T.sg, h), A.is_le,
+           ["#%d" % b, "sg%d" % h, "z%d" % (2 - 2 * h)], ["dg%d" % h])
 
     def diagonal_rows(h):
-        scan("ds%d" % h, part(T.ds, h), T.d0d[:], T.lt[:, 512 * h:512 * h + 512:4], A.mult, A.add, ["d0d", "dg%d" % h], ["ds%d" % h])
+        scan("ds%d" % h, part(T.ds, h), T.d0d[:], within[h], A.mult, A.add, ["d0d", "dg%d" % h], ["ds%d" % h])
 
     qx, sx = T.qx[:], T.sx[:]
     QX = ["qx0", "qx1"]
@@ -301,75 +320,108 @@ def rank_program(g, core, T, topo):
         for h in parts:
             hold("eh", T.eh, T.d0b, T.eo, h, ["d0b", "eo%d" % (h // 2)], ["eh%d" % h])
 
-    def served_colour(h):
-        mm("m2", bank(2, 0, 128), *side(T.qp, T.sp, 1), *side(T.qx, T.sx, h), ["qx%d" % h, "pc1", "ps1"], ["#2"])
-        act("cs%d" % h, part(T.tc, h), bank(2, 0, 128), F.Sign, ["#2", "cd2", "cd3"], ["tc%d" % h], scale=col(T.cd, 2), bias=col(T.cd, 3))
+    def colour_scores(h):
+        mm("m2", bank(2 - h, 0, 128), *side(T.qp, T.sp, 1), *side(T.qx, T.sx, h), ["qx%d" % h, "pc1", "ps1"], ["#%d" % (2 - h)])
 
-    def first_half():
-        mm("ma", bank(3, 0, 128), *side(T.qp, T.sp, 0), *side(T.qx, T.sx, 0), ["qx0", "pc0", "ps0"], ["#3"])
-        served_colour(0)
-        mm("mb", bank(1, 0, 128), *side(T.qp, T.sp, 0), *side(T.qx, T.sx, 0), ["qx0"], ["#1"])
+    def served_colour(h):
+        act("cs%d" % h, part(T.tc, h), bank(2 - h, 0, 128), F.Sign, ["#%d" % (2 - h), "cd2", "cd3"], ["tc%d" % h],
+            scale=col(T.cd, 2), bias=col(T.cd, 3))
+
+    def all_scores(b):
+        mm("m%d" % b, bank(b), *side(T.qp, T.sp, 0), qx, sx, QX + ["pc0", "ps0"], ["#%d" % b])
+
+    def half_scores(h, b):
+        mm("ma%d" % b, bank(b, 0, 128), *side(T.qp, T.sp, 0), *side(T.qx, T.sx, h), ["qx%d" % h, "pc0", "ps0"], ["#%d" % b])
+
+    def unpack():
+        for b in range(4):
+            mm("mf", bank(4 + b), *side(T.qe, T.se, b), qx, sx, QX + ["qe%d" % b], ["#%d" % (4 + b)])
+
+    def window_list(*pieces):
+        for h in pieces:
+            m = min(128, 544 - 128 * h)
+            scan("k20", T.tbh[:, 128 * h:128 * h + m], T.d0p[:, 0:m], T.tb[:, 128 * h:128 * h + m], A.add, A.max,
+                 ["d0p"] + ["tb%d" % j for j in range(4)], ["tbh%d" % h])
 
     for k in range(ROUNDS):
         first, last = k == 0, k == ROUNDS - 1
+        fused = 160 if last else 128
         if first:
-            quant("qx0", *side(T.qx, T.sx, 0), part(T.xin, 0, 512), ["xin0"], ["qx0"])
-            pick_codes("k13", 0)
             quant("qx1", *side(T.qx, T.sx, 1), part(T.xin, 1, 512), ["xin1"], ["qx1"])
-            pick_codes("k22", 1)
-            first_half()
-            scores(0, 3)
-        mm("m0", bank(0), *side(T.qp, T.sp, 0), qx, sx, QX + ["pc0", "ps0"], ["#0"])
-        hold("sg0", T.sg, T.d0g, T.sm, 0, ["d0g", "sm0"], ["sg0"])
-        cmp_rows(7, 6)
-        served_colour(1)
-        mm("m1", bank(1), *side(T.qp, T.sp, 0), qx, sx, QX, ["#1"])
-        for b in range(4):
-            mm("mf", bank(4 + b), *side(T.qe, T.se, b), qx, sx, QX + ["qe%d" % b], ["#%d" % (4 + b)])
-        if not first:
+            pick_codes(0)
+            quant("qx0", *side(T.qx, T.sx, 0), part(T.xin, 0, 512), ["xin0"], ["qx0"])
+            pick_codes(1)
+            half_scores(1, 2)
+            half_scores(0, 3)
+            all_scores(0)
+            all_scores(1)
+            scores(1)
+            scores(0)
+            mm("m2", bank(2), *side(T.qp, T.sp, 1), qx, sx, QX + ["pc1", "ps1"], ["#2"])
+            unit(3)
+            unpack()
+            held_scores(1)
+            held_scores(0)
+            cmp_rows(12, 11, 10)
+            act("cs0", T.tc[:], bank(2), F.Sign, ["#2", "cd2", "cd3"], ["tc0", "tc1"], scale=col(T.cd, 2), bias=col(T.cd, 3))
+            cmp(0, 15, 14)
+            diagonal(0, 3)
+            cmp(3, 7, 6, 5, 4, 3, 2, 1)
+            rows(15, 14)
+            cmp(0, 13)
+            quant("qa", T.qa[:], T.sa[:], T.wab[:], ["wab%d" % j for j in range(4)], ["qa"])
+            cmp(0, 9)
+            lower_counts(first)
+            diagonal(1, 0)
+            cmp(0, 8)
+            rows(7, 6, 5, 4, 3, 2, 1)
+            rows(13, 9, 8)
+        else:
+            half_scores(1, 2)
+            all_scores(0)
+            held_scores(0)
             offsets(0)
-        diagonal(0, 3)
-        cmp(3, 5)
-        scores(1, 0)
-        cmp(0, 4, 3)
-        hold("sg1", T.sg, T.d0g, T.sm, 1, ["d0g", "sm1"], ["sg1"])
-        rows(5, 4)
-        cmp(0, 2, 1)
-        cmp_rows(12, 10, 9)
-        cmp(0, 15, 14, 13)
-        diagonal(1, 0)
-        cmp(0, 11, 8)
-        rows(3, 2, 1, 15, 14, 13, 11, 8)
-        if first:
-            quant("k16", T.qa[:], T.sa[:], T.wab[:], ["wab%d" % j for j in range(4)], ["qa"])
-        pack("qla", 0, 256, lkeys(0))
-        count("mh", 2, 64, 192, "qla", start=True)
-        count("ml", 3, 0, 128, "qla", start=True)
-        pack("qlb", 256, 576 if first else 512, lkeys(1) + lkeys(3) + ["z4"])
-        count("mh", 2, 256 + 64, 128, "qlb", stop=True)
-        count("ml", 3, 256, 128, "qlb")
-        count("ml", 3, 448, 128, "qlb")
-        pack("qlc", 576, 704, lkeys(2))
-        count("ml", 3, 576, 128, "qlc", stop=True)
+            cmp(3, 5, 4, 3)
+            cmp_rows(7, 6)
+            all_scores(1)
+            scores(1)
+            unpack()
+            cmp(3, 2, 1)
+            diagonal(0, 3)
+            held_scores(1)
+            rows(5, 4, 3, 2, 1)
+            cmp_rows(12, 11)
+            colour_scores(1)
+            lower_counts(first)
+            cmp(0, 10, 9, 15, 14)
+            rows(10, 9, 15, 14)
+            cmp(0, 13)
+            diagonal(1, 0)
+            cmp(0, 8)
+            rows(13, 8)
+            served_colour(1)
+        upper_counts(first)
         diagonal_rows(0)
         diagonal_rows(1)
         if first:
             offsets(0)
-            ts("k23", T.msel[:], T.m2[:], col(T.cf, PAR8), 2.0 ** 21, A.subtract, A.mult, ["m2", "cf"], ["msel"])
-            column("k24", 4, PAR8, -2.0 ** 19, 2.0 ** 22)
-        scan("hp1", part(T.hp, 1), T.d0p[:], bank(2, 64, 192), A.add, A.max, ["d0p", "#2"], ["hp1"])
+            act("k13", T.d0s[:], T.a16w[:, 0:280], F.Abs, ["a16w", "cf"], ["d0s"], scale=-1.0, bias=col(T.cf, PAR8))
+            column("k14", 0, LAST, -2.0 * STEP, STEP)
+            column("k14", 4, PAR8, -24.0 * STEP, 192.0 * STEP)
+            column("k14", 11, PAR8, -96.0 * STEP, 0.0)
+            column("k14", 6, R, 2.0, 34.5)
+            column("k14", 7, R, 512.0, -7680.0)
+            act("k15", col(T.d0s, 256), col(T.a16w, 0), F.Identity, ["d0s"], ["d0s"])
+            act("k12", T.msel[:], T.m2[:], F.Identity, ["m2", "cd11"], ["msel"], scale=96.0 * STEP, bias=col(T.cd, 11))
+            act("k16", T.d0s[:], T.d0s[:], F.Relu, ["d0s"], ["d0s"], scale=-1.0, bias=1.0)
+            act("k21", col(T.msel, 31), col(T.cd, 0), F.Identity, ["cd0", "cd4", "msel"], ["msel"], scale=col(T.cf, PAR8), bias=col(T.cd, 4))
+            act("k17", T.d0s[:], T.d0s[:], F.Identity, ["d0s", "cd0"], ["d0s"], scale=-2.0 ** 25, bias=col(T.cd, 0))
         tt("dc", T.pre[:, 0:16], T.ds[:, 15:256:16], T.kt[:], A.add, ["ds0", "ds1", "kt"], ["dc"])
+        scan("hp1", part(T.hp, 1), T.d0p[:], bank(2, 0, 128), A.add, A.max, ["d0p", "#2"], ["hp1"])
         scan("hp0", part(T.hp, 0), T.d0p[:], bank(3, 0, 128), A.add, A.max, ["d0p", "#3"], ["hp0"])
         tt("pre", T.pre[:, 16:32], T.rs[:], T.pre[:, 0:16], A.add, ["dc"] + ["rs%d" % t for t in range(16)], ["pre"])
         offsets(1)
         tt("lp", T.lp[:], T.hp[:, 15:256:16], T.pre[:, 16:32], A.subtract, ["hp0", "hp1", "pre"], ["lp"])
-        if first:
-            act("k26", T.d0s[:], T.a16w[:, 0:280], F.Abs, ["a16w", "cf"], ["d0s"], scale=-1.0, bias=col(T.cf, PAR8))
-            act("k27", col(T.d0s, 256), col(T.a16w, 0), F.Identity, ["d0s"], ["d0s"])
-            act("k28", T.d0s[:], T.d0s[:], F.Relu, ["d0s"], ["d0s"], scale=-1.0, bias=1.0)
-            act("k29", T.d0s[:], T.d0s[:], F.Identity, ["d0s", "cd0"], ["d0s"], scale=-2.0 ** 25, bias=col(T.cd, 0))
-            ts("k30", col(T.msel, 31), col(T.cd, 0), col(T.cf, PAR8), col(T.cd, 4), A.mult, A.add, ["cd0", "cd4", "msel"], ["msel"])
-            column("k31", 6, R, 2.0, 34.5)
         for b in (0, 2, 1, 3):
             o = 528 * (b % 2) + 1 + 257 * (b // 2)
             act("f%d" % (b % 2), T.f2[:, o:o + 256], bank(4 + b), F.Copy, ["#%d" % (4 + b)], ["f%d" % b])
@@ -380,29 +432,30 @@ def rank_program(g, core, T, topo):
         scan("na", T.na[:, 256:280], T.d0s[:, 256:280], T.xo[:, 0:24], A.add, A.max, ["d0s", "xo"], ["nb"])
         scan("na", T.na[:, 0:256], T.d0s[:, 0:256], T.xo[:], A.add, A.max, ["d0s", "xo"], ["na"])
         ts("w1", wi(1), wi(0), 2, 62, A.logical_shift_right, A.bitwise_and, ["w0"], ["w1"])
-        scan("s1", T.s1[:], T.msel[:], T.na[:, 15:280:8], A.add, A.max, ["na", "nb", "msel"], ["s1"])
         ts("w2", wi(2), wi(0), 3, 1, A.logical_shift_right, A.bitwise_and, ["w0"], ["w2"])
-        ts("s2", T.s2[:, 0:17], T.s1[:, 1:34:2], 1.5 * 2.0 ** 34, 1.5 * 2.0 ** 34, A.add, A.subtract, ["s1"], ["s2"])
+        for out in (T.s1, T.s2):
+            scan("s1", out[:], T.msel[:], T.na[:, 15:280:8], A.add, A.max, ["na", "nb", "msel"], [out.name])
         ts("w3", wf(0), wi(1), col(T.cd, 6), None, A.add, None, ["w1", "cd6"], ["base"])
-        tt("l1", T.l1[:, 0:17], T.s1[:, 1:34:2], T.s2[:, 0:17], A.subtract, ["s1", "s2"], ["l1"])
+        tt("l1", T.l1[:, 0:17], T.s1[:, 1:34:2], T.s2[:, 1:34:2], A.subtract, ["s1", "s2"], ["l1"])
         ts("w4", wf(1), wi(2), 63.5, -31.5, A.mult, A.add, ["w2"], ["ce"])
-        act("g1", T.gz[:, 272:544], T.f2[:, 528:1042].indirect(T.l1[:, 0:17]), F.Copy, ["l1", "f1", "f3", "f2z"], ["g1"], scale=0.25)
-        ts("g0", T.gz[:, 0:272], T.f2[:, 0:514].indirect(T.l1[:, 0:17]), 0.25, None, A.mult, None, ["l1", "f0", "f2", "f2y"], ["g0"])
         ts("w4", wf(2), wi(2), -63.5, 32.0, A.mult, A.add, ["w2"], ["co"])
-        if first:
-            late_constants()
-            pick_scales("k32", 2)
-            pick_scales("k33", 3)
-            act("k34", T.d0b[:], T.own[:], F.Identity, ["own"], ["d0b"], scale=-260.0 / BIG, bias=-256.0)
-        for w in range(2):
-            o = 272 * w
-            scan("zz%d" % w, T.zz[:, o:o + 272], T.alt[:], T.gz[:, o:o + 272], A.mult, A.add, ["alt", "g%d" % w], ["zz%d" % w])
-        for w in range(2):
-            o = 272 * w
-            tt("y", T.yt[:, w:264:2], T.zz[:, o + 1:o + 264:2], T.zz[:, o + 9:o + 272:2], A.add, ["zz%d" % w], ["y%d" % w])
+        for h in range(2):
+            act("g1%d" % h, part(T.gz, 2 + h, 144), T.f2[:, 528:1042].indirect(T.l1[:, 8 * h:8 * h + 9]), F.Copy,
+                ["l1", "f1", "f3", "f2z"], ["g1%d" % h], scale=0.25)
+            ts("g0%d" % h, part(T.gz, h, 144), T.f2[:, 0:514].indirect(T.l1[:, 8 * h:8 * h + 9]), 0.25, None, A.mult, None,
+               ["l1", "f0", "f2", "f2y"], ["g0%d" % h])
+        for h in range(2):
+            for w in range(2):
+                i = 2 * w + h
+                scan("zz%d" % h, part(T.zz, i, 144), T.alt[:], part(T.gz, i, 144), A.mult, A.add, ["alt", "g%d%d" % (w, h)], ["zz%d" % i])
+        for h in range(2):
+            for w in range(2):
+                i, m = 2 * w + h, 128 + 8 * h
+                tt("y", T.yt[:, 128 * h + w:128 * h + m:2], T.zz[:, 144 * i + 1:144 * i + m:2], T.zz[:, 144 * i + 9:144 * i + 8 + m:2], A.add,
+                   ["zz%d" % i], ["y%d" % i])
         if not first:
             held_colours(0, 1)
-        quant("qy", *side(T.qy, T.sy, k), T.yt[:], ["y0", "y1", "ytz"], ["qy%d" % k])
+        quant("qy", *side(T.qy, T.sy, k), T.yt[:], ["y0", "y1", "y2", "y3", "ytz"], ["qy%d" % k])
         a, c = LAND[k], 128 * k
         arr = T.sem["arr%d" % k]
         op("g", None, lambda a=a, c=c, arr=arr: g.remote_dma(
@@ -410,32 +463,38 @@ def rank_program(g, core, T, topo):
         op("g", None, lambda a=a, c=c, arr=arr: g.remote_dma(
             T.ls[:, a:a + NY], T.sy[:, c:c + NY], arr, T.sem.sent, pid, rid, topo.mask(core, nxt)), [])
         if first:
-            later_constants()
-            pick_codes("k35", 2)
-            pick_codes("k36", 3)
+            for j in range(3):
+                iota("i13", part(T.ndt, j), [[1, 64], [j + 1, 2]], 0, 0, ["ndt%d" % j])
+            iota("i14", T.ndt[:, 127:254:126], [[0, 2]], 0, 0, ["ndt0", "ndt1"])
+            iota("i15", T.ndt[:, 255:382:126], [[0, 2]], 1, 0, ["ndt1", "ndt2"])
+            pick_codes(2)
+            pick_codes(3)
+            window_list(0, 1, 2, 3, 4)
+            pick_scales(2)
+            pick_scales(3)
+            act("k19", T.d0b[:], T.own[:], F.Identity, ["own"], ["d0b"], scale=-260.0 / BIG, bias=-256.0)
+            act("k22", col(T.cd, 8), col(T.cf, COL4), F.Identity, ["cf"], ["cd8"], bias=col(T.cf, PAR8))
+            column("k22", 10, R, 34.0, -1548.0)
+            column("k22", 14, R, 4.0, -60.0)
+            for h in range(2):
+                blank("k23", part(T.zt, h, 256), 256, ["zt%d" % h])
+            act("k24", T.a4[:], T.a4[:], F.Abs, ["a4", "cd8"], ["a4"], scale=-1.0, bias=col(T.cd, 8))
+            act("k25", col(T.cd, 13), col(T.cd, 8), F.Identity, ["cd8", "cd10"], ["cd13"], scale=95.0, bias=col(T.cd, 10))
+            blank("k25", T.ht[:, 264:512], 248, ["htz"])
+            act("k26", T.a4[:], T.a4[:], F.Sign, ["a4"], ["a4"])
             colours()
-            op("v", "k37", lambda: V.memset(T.zt[:], 0.0), (), ["zt"])
-            for h in range(4):
-                hold("k38", T.tbh, T.d0p, T.tb, h, ["tb%d" % j for j in range(4)], ["tbh%d" % h])
-            scan("k38", T.tbh[:, 512:544], T.d0p[:, 0:32], T.tb[:, 512:544], A.add, A.max, ["tb3"], ["tbh4"])
-            quant("k39", T.lc[:, 208:336], T.ls[:, 208:336], T.zt[:], ["zt"], ["lz"])
-            column("k40", 7, R, 512.0, -7680.0)
-            act("k40", col(T.cd, 8), col(T.cf, COL4), F.Identity, ["cf"], ["cd8"], bias=col(T.cf, PAR8))
-            column("k40", 10, R, 34.0, -1548.0)
-            column("k40", 14, R, 4.0, -60.0)
-            act("k44", col(T.cd, 13), col(T.cd, 8), F.Identity, ["cd8", "cd10"], ["cd13"], scale=95.0, bias=col(T.cd, 10))
-            act("k46", T.a4[:], T.a4[:], F.Abs, ["a4", "cd8"], ["a4"], scale=-1.0, bias=col(T.cd, 8))
-            act("k47", T.a4[:], T.a4[:], F.Sign, ["a4"], ["a4"])
-            act("k48", T.d0c[:], T.a4[:], F.Identity, ["a4"], ["d0c"], scale=260.0, bias=-256.0)
-            act("k48", T.d0l[:], T.a4[:], F.Identity, ["a4"], ["d0l"], scale=66048.0, bias=-65536.0)
-            ts("k49", T.lw[:], T.tbh[:, 15:544:16], col(T.cd, 7), None, A.add, None, ["cd7"] + ["tbh%d" % h for h in range(5)], ["lw"])
+            quant("lz", T.lc[:, 208:336], T.ls[:, 208:336], T.zt[:], ["zt0", "zt1"], ["lz"])
+            ts("k28", T.lw[:], T.tbh[:, 15:544:16], col(T.cd, 7), None, A.add, None, ["cd7"] + ["tbh%d" % h for h in range(5)], ["lw"])
             held_colours(0, 1)
         held_colours(2, 3)
         for b in range(4):
-            act("fi", T.fi[:, b:4 * NA:4], bank(4 + b, 0, NA), F.Copy, ["#%d" % (4 + b)], ["fi%d" % b])
+            act("fi", T.fi[:, b:4 * fused:4], bank(4 + b, 0, fused), F.Copy, ["#%d" % (4 + b)], ["fi%d" % b])
+        if first:
+            act("k27", T.d0c[:], T.a4[:], F.Identity, ["a4"], ["d0c"], scale=260.0, bias=-256.0)
+            act("k27", T.d0l[:], T.a4[:], F.Identity, ["a4"], ["d0l"], scale=66048.0, bias=-65536.0)
         tt("w5", wf(3, 2), T.eh[:, 15:512:16], wf(1, 2), A.mult, ["eh%d" % h for h in range(4)] + ["ce", "co"], ["w5"])
         if k == 1:
-            quant("k50", T.qv[:], T.sv[:], T.vt[:], ["vt"], ["qv"])
+            quant("qv", T.qv[:], T.sv[:], T.vt[:], ["vt"], ["qv"])
         tt("w6", wf(5), wf(3), wf(0), A.add, ["w5", "base"], ["w6"])
         tt("w7", T.lcb[:], wf(5), wf(4), A.add, ["w5", "w6"], ["lcb"])
         act("lob", T.lob[:], T.ptab[:, 0:192].indirect(T.lcb[:]), F.Copy, ["lcb", "ptab0", "ptab1", "ptab2"], ["lob"])
@@ -458,7 +517,7 @@ def rank_program(g, core, T, topo):
             hold("l4", T.l4, T.d0l, T.lob, h, ["d0l", "lob"], ["l4%d" % h])
         cp("vs", T.vs[:], bank(0, 0, NY), ["#0"], ["vs"])
         ts("lo4", T.lo4[:], T.l4[:, 3:256:4], col(T.cd, 13), None, A.add, None, ["l40", "l41", "cd13"], ["lo4"])
-        tt("d", T.dtb[:, 1:64:2], T.vs[:, 1:64:2], bank(0, 2, 65, 2), A.subtract, ["#0", "vs"], ["d1"])
+        scan("d", T.dtb[:, 0:64], T.flip[:], bank(0, 1, 65), A.mult, A.subtract, ["#0", "flip"], ["d1"])
         tt("d", T.dtb[:, 64:128], T.vs[:, 0:64], bank(0, 2, 66), A.subtract, ["#0", "vs"], ["d2"])
         tt("d", T.dtb[:, 128:192:2], T.vs[:, 0:63:2], bank(0, 3, 66, 2), A.subtract, ["#0", "vs"], ["d3"])
         for h in range(2):
@@ -466,42 +525,55 @@ def rank_program(g, core, T, topo):
                ["d1", "d2", "d3", "lcb", "th"], ["bt%d" % h])
         for h in range(2):
             hold("bh%d" % h, T.bh, T.d0c, T.bt, h, ["d0c", "bt%d" % h], ["bh%d" % h])
+            if last and h == 0:
+                hold("b16", T.b16, T.d0b, T.bt, 0, ["bt0"], ["b160"])
         for h in range(2):
             tt("lh%d" % h, part(T.lh, h, 32), T.bh[:, 128 * h + 3:128 * h + 128:4], part(T.lo4, h, 32), A.add, ["bh%d" % h, "lo4"], ["lh%d" % h])
-        for q in range(2):
-            act("gh%d" % q, part(T.gh, q, 256), T.hw[:, 0:544].indirect(part(T.lh, 2 + q, 16)), F.Copy, ["lh1", "hw"], ["gh%d" % q])
-        tt("xa", part(T.xs, 0, 512), T.hw[:, 0:544].indirect(part(T.lh, 0, 32)), T.fi[:], A.add,
-           ["lh0", "hw"] + ["fi%d" % b for b in range(4)], ["xa"])
+            if last and h == 0:
+                hold("b16", T.b16, T.d0b, T.bt, 1, ["bt1"], ["b161"])
+        cuts = [fused, 256] if last else [fused, 192, 256]
+        for q in range(len(cuts) - 1):
+            act("gh%d" % q, T.gh[:, 4 * cuts[q] - 512:4 * cuts[q + 1] - 512], T.hw[:, 0:544].indirect(T.lh[:, cuts[q] // 4:cuts[q + 1] // 4]),
+                F.Copy, ["lh1", "hw"], ["gh%d" % q])
+        FI = ["hw"] + ["fi%d" % b for b in range(4)]
+        tt("xa", part(T.xs, 0, 512), T.hw[:, 0:544].indirect(part(T.lh, 0, 32)), T.fi[:, 0:512], A.add, ["lh0"] + FI, ["xa"])
 
         def rest(*pieces):
             for i in pieces:
                 q, b = divmod(i, 4)
-                tt("x", T.xs[:, 512 + 256 * q + b:768 + 256 * q:4], bank(4 + b, 128 + 64 * q, 192 + 64 * q), T.gh[:, 256 * q + b:256 * q + 256:4],
+                c0, c1 = cuts[q], cuts[q + 1]
+                tt("x", T.xs[:, 4 * c0 + b:4 * c1:4], bank(4 + b, c0, c1), T.gh[:, 4 * c0 - 512 + b:4 * c1 - 512:4],
                    A.add, ["#%d" % (4 + b), "gh%d" % q], ["x%d" % i])
-        rest(0, 1)
-        quant("qx0", *side(T.qx, T.sx, 0), part(T.xs, 0, 512), ["xa"], ["qx0"])
-        if last:
-            mm("ma", bank(3, 0, 128), T.qv[:], T.sv[:], *side(T.qx, T.sx, 0), ["qx0", "qv"], ["#3"])
-        else:
-            first_half()
-        rest(2, 3, 4, 5, 6, 7)
-        if last:
-            for h in range(2):
-                hold("b16", T.b16, T.d0b, T.bt, h, ["bt%d" % h], ["b16%d" % h])
-        else:
-            scores(0, 3)
-        quant("qx1", *side(T.qx, T.sx, 1), part(T.xs, 1, 512), ["x%d" % b for b in range(8)], ["qx1"])
 
-    tt("ln", T.ln[:], T.b16[:, 15:256:16], wf(6), A.add, ["b160", "b161", "lo16"], ["ln"])
+        def packed(h):
+            quant("qx%d" % h, *side(T.qx, T.sx, h), part(T.xs, h, 512), ["x%d" % b for b in range(8)] if h else ["xa"], ["qx%d" % h])
+        if last:
+            tt("ln", T.ln[:], T.b16[:, 15:256:16], wf(6), A.add, ["b160", "b161", "lo16"], ["ln"])
+            act("nd", T.ndf[:], T.ndt[:, 0:384].indirect(T.ln[:]), F.Copy, ["ln", "ndt0", "ndt1", "ndt2"], ["ndf"])
+            dma("a", "out", T.nd[:], T.ndf[0:128:16, :], ["ndf"], ["o0"])
+            tt("x", T.xs[:, 512:4 * fused], T.hw[:, 0:544].indirect(T.lh[:, 32:fused // 4]), T.fi[:, 512:4 * fused], A.add, ["lh1"] + FI, ["x7"])
+            rest(0, 1, 2, 3)
+            packed(0)
+            mm("ma3", bank(3, 0, 128), T.qv[:], T.sv[:], *side(T.qx, T.sx, 0), ["qx0", "qv"], ["#3"])
+            packed(1)
+        else:
+            rest(0, 1)
+            packed(0)
+            half_scores(0, 3)
+            colour_scores(0)
+            half_scores(0, 1)
+            served_colour(0)
+            rest(2, 3, 4, 5, 6, 7)
+            scores(0)
+            packed(1)
+
     mm("m1", bank(1, 0, 128), T.qv[:], T.sv[:], *side(T.qx, T.sx, 1), ["qx1", "qv"], ["#1"])
     dma("s", "out", part(T.oc, 0, 512), part(T.qx, 0).bitcast(dt.uint8), ["qx0"], ["o1"])
     act("cs0", part(T.yo, 0), bank(3, 0, 128), F.Copy, ["#3"], ["yo0"])
     dma("a", "out", part(T.y, 0), part(T.yo, 0), ["yo0"], ["o2"])
-    act("nd", T.ndf[:], T.ndt[:, 0:384].indirect(T.ln[:]), F.Copy, ["ln", "ndt0", "ndt1", "ndt2"], ["ndf"])
     dma("s", "out", part(T.oc, 1, 512), part(T.qx, 1).bitcast(dt.uint8), ["qx1"], ["o3"])
     for j in range(4):
         dma("sa"[j // 3], "out", T.osc[4 * j:4 * j + 4, :], T.sx[32 * j:32 * j + 4, :], QX, ["o%d" % (4 + j)])
-    dma("a", "out", T.nd[:], T.ndf[0:128:16, :], ["ndf"], ["o0"])
     cp("yo", part(T.yo, 1), bank(1, 0, 128), ["#1"], ["yo1"])
     dma("s", "out", part(T.y, 1), part(T.yo, 1), ["yo1"], ["o8"])
     op("g", None, None, ["o%d" % j for j in range(9)], ext=(T.sem.sent, 2 * ROUNDS * len(topo.engines(core, nxt))))

from concourse.mybir import dt, AluOpType, ActivationFunctionType

A = AluOpType
F = ActivationFunctionType
C4, U8, BF, F32, I32, U16 = "float8_e4m3fn_x4", "uint8", "bfloat16", "float32", "int32", "uint16"
ROUNDS = 3
NY = 66
LAND = [142, 76, 10]
TILES = [0, 256, 512, 640]
STEP = 8192.0
TINY, BIG = 2.0 ** -100, 2.0 ** 90


def _s(n, d):
    return ("sbuf", [128, n], d)


SCRATCH = {
    "ps": ("psum", [128, 4096], F32),
    "xin": _s(1024, BF), "ut": _s(512, BF), "vt": _s(512, BF), "xs": _s(1024, BF),
    "qu": _s(128, C4), "su": _s(128, U8), "qp": _s(512, C4), "sp": _s(512, U8),
    "qv": _s(128, C4), "sv": _s(128, U8), "qw": _s(512, C4), "sw": _s(512, U8),
    "qx": _s(256, C4), "sx": _s(256, U8), "qe": _s(512, C4), "se": _s(512, U8),
    "qa": _s(128, C4), "sa": _s(128, U8), "ql": _s(768, C4), "sl": _s(768, U8),
    "qy": _s(384, C4), "sy": _s(384, U8), "lc": _s(336, C4), "ls": _s(336, U8),
    "qh": _s(128, C4), "sh": _s(128, U8),
    "pi": _s(8, I32), "ci": _s(8, I32), "cf": _s(8, F32), "cd": _s(16, F32), "lpi": _s(24, I32), "lpk": _s(32, U16),
    "a16": _s(128, F32), "a16w": _s(288, F32), "a4": _s(128, F32), "gv": _s(128, F32), "d128": _s(128, F32),
    "jr": _s(256, F32), "jt": _s(256, F32), "kt": _s(16, F32), "flip": _s(64, F32),
    "m2": _s(34, F32), "msel": _s(34, F32), "alt": _s(144, BF), "nt": _s(192, F32), "zt": _s(512, BF),
    "own": _s(128, F32), "d0g": _s(128, F32), "d0d": _s(128, BF), "d0p": _s(128, F32), "d0b": _s(128, BF),
    "d0c": _s(128, BF), "d0l": _s(128, F32), "d0s": _s(280, F32), "eb": _s(520, BF), "wab": _s(512, BF),
    "tb": _s(544, F32), "tbh": _s(544, F32), "lw": _s(34, U16), "ptab": _s(192, F32), "ndt": _s(384, F32),
    "sm": _s(256, F32), "sg": _s(256, F32), "tc": _s(256, BF), "sgn": _s(1920, BF),
    "lt": _s(3072, BF), "jk": _s(1920, BF), "rs": _s(16, F32),
    "ds": _s(256, BF), "pre": _s(32, F32), "hp": _s(256, F32), "lp": _s(16, U16),
    "xv": _s(256, F32), "xo": _s(256, F32), "na": _s(280, F32), "s1": _s(34, F32), "s2": _s(34, BF),
    "l1": _s(18, U16), "f2": _s(1056, BF), "fi": _s(640, BF), "gz": _s(576, BF), "zz": _s(576, BF),
    "yt": _s(512, BF), "eo": _s(512, BF), "eh": _s(512, BF), "wi": _s(48, I32), "wf": _s(128, F32),
    "lcb": _s(16, U16), "th": _s(256, F32), "lob": _s(256, F32), "l4": _s(256, F32), "lo4": _s(64, F32),
    "ht": _s(512, BF), "hw": _s(544, BF), "vs": _s(66, F32),
    "dtb": _s(192, F32), "bt": _s(256, BF), "bh": _s(256, BF), "b16": _s(256, BF), "lh": _s(64, U16), "ln": _s(16, U16),
    "gh": _s(512, BF), "ndf": _s(256, F32), "yo": _s(256, F32),
}
NSEM = 140
SEMAPHORES = ["s%d" % i for i in range(NSEM)] + ["sent", "arr0", "arr1", "arr2"]


def rank_program(g, core, T, topo):
    rank = T.rank_of(core)
    if rank is None:
        return
    n = len(T.cores)
    nxt, prv = T.cores[(rank + 1) % n], T.cores[(rank - 1) % n]
    V, S, P = g.vector, g.scalar, g.tensor
    queue = {"g": g, "v": V, "a": S, "p": P, "s": g.sync}

    ops, lastw, readers, tags = [], {}, {}, {}
    know = {q: 0 for q in queue}

    def op(q, tag, fn, r=(), w=(), inc=1, acc=False, ext=None):
        deps = set()
        for k in r:
            if k in lastw:
                deps.add(lastw[k])
            if k[0] == "#":
                deps.update(o for o in readers.get(k, ()) if ops[o]["q"] != q)
        for k in w:
            if k in lastw and not acc:
                deps.add(lastw[k])
            deps.update(readers.get(k, ()))
        t = tags.setdefault(tag, {"ops": [], "closed": 0}) if tag else None
        waits = []

        def need(d):
            if know[q] >> d & 1:
                return
            td = tags[ops[d]["tag"]]
            td["closed"] = len(td["ops"])
            waits.append((ops[d]["tag"], sum(ops[o]["inc"] for o in td["ops"])))
            for o in td["ops"]:
                know[q] |= ops[o]["know"] | 1 << o
        for d in sorted(deps, reverse=True):
            need(d)
        if t:
            for d in t["ops"][:t["closed"]]:
                need(d)
        me = len(ops)
        ops.append({"q": q, "tag": tag, "fn": fn, "inc": inc, "waits": waits, "ext": ext, "know": know[q]})
        if t:
            t["ops"].append(me)
        for k in r:
            readers.setdefault(k, []).append(me)
        for k in w:
            lastw[k] = me
            readers[k] = []

    def bank(b, a=0, e=256, s=1):
        return T.ps[:, 512 * b + a:512 * b + e:s]

    def ts(tag, out, in0, s1, s2, o0, o1, r, w):
        if o1 is None:
            op("v", tag, lambda: V.tensor_scalar(out, in0, s1, None, o0), r, w)
        else:
            op("v", tag, lambda: V.tensor_scalar(out, in0, s1, s2, o0, o1), r, w)

    def tt(tag, out, a, b, o, r, w):
        op("v", tag, lambda: V.tensor_tensor(out, a, b, o), r, w)

    def cp(tag, out, a, r, w):
        op("v", tag, lambda: V.tensor_copy(out, a), r, w)

    def scan(tag, out, d0, d1, o0, o1, r, w):
        op("v", tag, lambda: V.tensor_tensor_scan(out, d0, d1, 0.0, o0, o1), r, w)

    def act(tag, out, a, f, r, w, **kw):
        op("a", tag, lambda: S.activation(out, a, f, **kw), r, w)

    def quant(tag, q, s, a, r, w):
        op("v", tag, lambda: V.quantize_mx(q, s, a), r, w)

    def mm(tag, out, lq, lsc, rq, rsc, r, w, start=True, stop=True, ext=None):
        op("p", tag, lambda: P.matmul_mx(out, lq, lsc, rq, rsc, start, stop), r, w, acc=not start, ext=ext)

    def iota(tag, out, pat, base, cm, w, small=True):
        if small:
            op("g", tag, lambda: g.iota(out, pat, base, cm, allow_small_or_imprecise_dtypes=True), (), w)
        else:
            op("g", tag, lambda: g.iota(out, pat, base, cm), (), w)

    def zero(tag, out, m, w):
        iota(tag, out, [[0, m]], 0, 0, w)

    def dma(q, tag, out, a, r, w):
        op(q, tag, lambda: queue[q].dma_start(out, a), r, w, inc=16)

    def col(t, j):
        return t[:, j:j + 1]

    def part(t, h, m=128):
        return t[:, m * h:m * h + m]

    def side(q, s, b):
        return part(q, b), part(s, b)

    def pick_list(b):
        return part(T.lpk, [0, 3, 1, 2][b], 8)

    def pick_codes(b):
        cp("pc%d" % b, part(T.qp, b).bitcast(dt.uint32), T.qu[:, 0:128].bitcast(dt.uint32).indirect(pick_list(b)),
           ["qu", "lpk%d" % b], ["pc%d" % b])

    def pick_scales(b):
        act("ps%d" % b, part(T.sp, b), T.su[:, 0:128].indirect(pick_list(b)), F.Copy, ["qu", "lpk%d" % b], ["ps%d" % b])

    def column(tag, j, src, sc, bi):
        if isinstance(bi, int):
            act(tag, col(T.cd, j), col(T.cf, src), F.Identity, ["cf", "cd%d" % bi], ["cd%d" % j], scale=sc, bias=col(T.cd, bi))
        else:
            act(tag, col(T.cd, j), col(T.cf, src), F.Identity, ["cf"], ["cd%d" % j], scale=sc, bias=bi)

    def hold(tag, out, d0, a, h, r, w):
        scan(tag, part(out, h), d0[:], part(a, h), A.add, A.max, r, w)

    def unit(b):
        quant("qe%d" % b, *side(T.qe, T.se, b), T.eb[:, 3 - b:515 - b], ["eb"], ["qe%d" % b])

    def blank(tag, out, m, w):
        act(tag, out, T.eb[:, 0:2 * m:2], F.Copy, ["eb0"], w)

    dma("a", "ldu", T.ut[:], T.u[:], [], ["ut"])
    for h in (1, 0):
        dma("s", "ldx%d" % h, part(T.xin, h, 512), part(T.x, h, 512), [], ["xin%d" % h])
    dma("s", "ldw", T.qw[:].bitcast(dt.uint8), T.wc[:], ["xin0", "xin1"], ["qw"])
    dma("s", "ldw", T.sw[:], T.ws[:], [], ["sw"])
    dma("s", "ldv", T.vt[:], T.v[:], [], ["vt"])

    R, PAR8, COL4, PAIR2, LAST = range(5)
    iota("i0", T.pi[:], [[0, 8]], 0, 1, ["pi"], False)
    iota("i1", T.d128[:], [[1, 128]], 0, -1, ["d128"])
    iota("i2", T.lpi[:], [[8, 3], [128, 8]], 0, 0, ["lpi"], False)
    iota("i3", T.a16[:], [[0, 8], [1, 16]], 0, 0, ["a16"])
    iota("i4", T.gv[:], [[16, 8], [0, 16]], 0, -1, ["gv"])
    iota("i5", T.jr[:], [[1, 256]], 16 * int(STEP) + 1, 0, ["jr"])
    zero("z3", T.lt[:, 4 * 656:4 * 704], 192, ["z3"])
    zero("z4", T.lt[:, 4 * 704:4 * 768], 256, ["z4"])
    zero("z5", T.lt[:, 4 * 448:4 * 512], 256, ["z5"])
    zero("i6", T.rs[:, 0:1], 1, ["rs0"])
    iota("i6", T.m2[:], [[0, 17], [8, 2]], -6, 0, ["m2"])
    iota("i7", T.a16w[:], [[0, 18], [1, 16]], 0, 0, ["a16w"])
    for j, (pat, base) in enumerate([([[1, 4], [8, 34]], 0), ([[1, 4], [8, 34]], 4),
                                     ([[1, 4], [16, 17], [12, 2]], 0), ([[1, 4], [16, 17], [4, 2]], 4)]):
        iota("i8", part(T.tb, j, 136), pat, base, 0, ["tb%d" % j])
    iota("i9", T.a4[:], [[0, 32], [4, 4]], 0, 0, ["a4"])
    zero("i10", T.f2[:, 0:258:257], 2, ["f2y"])
    zero("i10", T.f2[:, 528:786:257], 2, ["f2z"])
    zero("i10", T.yt[:, 264:512], 248, ["ytz"])
    iota("i10", T.alt[:], [[0, 72], [1, 2]], 0, 0, ["alt"])
    for j, (pat, base) in enumerate([([[2, 16], [-135, 2], [0, 2]], 408), ([[1, 32], [136, 2]], 0), ([[2, 16], [137, 2], [0, 2]], 272)]):
        iota("i11", part(T.ptab, j, 64), pat, base, 0, ["ptab%d" % j])
    iota("i12", T.flip[:], [[0, 32], [-1, 2]], 0, 0, ["flip"])
    zero("i12", T.dtb[:, 128:192], 64, ["d3"])
    iota("i12", T.nt[:], [[0, 3], [1, 64]], 0, 0, ["nt"])

    op("v", "k0", lambda: V.memset(T.eb[:], 0.0), (), ["eb", "eb0"])
    for j, m in enumerate([15, 8, 4, 2, 1]):
        ts("k1", col(T.ci, j), col(T.pi, j), m, None, A.bitwise_and, None, ["pi"], ["ci%d" % j])
    ts("k2", T.eb[:, 3:515:4], T.d128[:], 0.0, None, A.is_equal, None, ["d128"], ["eb"])
    cp("k3", T.cf[:, 0:5], T.ci[:, 0:5], ["ci%d" % j for j in range(5)], ["cf"])
    for j, e in enumerate([256, 448, 640]):
        blank("z%d" % j, T.lt[:, 4 * e - 192:4 * e], 192, ["z%d" % j])
    ts("k4", T.lpk[:, 0:24], T.lpi[:], 0.125, None, A.mult, None, ["lpi"], ["lpk0", "lpk2", "lpk3"])
    unit(0)
    unit(1)
    ts("k4", T.lpk[:, 24:32], T.lpi[:, 8:16], col(T.cf, PAR8), 0.125, A.add, A.mult, ["lpi", "cf"], ["lpk1"])
    ts("k5", T.own[:], T.a16[:], col(T.cf, R), -BIG, A.not_equal, A.mult, ["a16", "cf"], ["own"])
    unit(2)
    quant("qu", T.qu[:], T.su[:], T.ut[:], ["ut"], ["qu"])
    column("k7", 2, COL4, 0.5, -1.0)
    column("k7", 3, COL4, -0.5 * TINY, TINY)
    column("k7", 9, PAR8, 22.0 * STEP, 0.0)
    column("k7", 5, R, -511.0, 7665.0)
    act("k9", T.d0d[:], T.a16[:], F.Sign, ["a16"], ["d0d"])
    column("k9", 1, PAIR2, 128.5, 9)
    act("k9", T.kt[:], T.a16[:, 0:16], F.Identity, ["a16", "cd5"], ["kt"], scale=-16.0, bias=col(T.cd, 5))
    act("k6", T.gv[:], T.gv[:], F.Abs, ["gv"], ["gv"], bias=7.5)
    act("k6", T.d0g[:], T.d0d[:], F.Identity, ["d0d"], ["d0g"], scale=2 * BIG, bias=-2 * BIG)
    pick_scales(0)
    act("k8", T.gv[:], T.gv[:], F.Relu, ["gv"], ["gv"], scale=-1.0, bias=8.0)
    pick_scales(1)
    for j in range(4):
        act("k10", T.wab[:, j:512:4], T.gv[:], F.Sign, ["gv"], ["wab%d" % j])
    act("k11", T.d0p[:], T.own[:], F.Identity, ["own"], ["d0p"], scale=-66048.0 / BIG, bias=-65536.0)
    act("k11", T.jt[:], T.jr[:], F.Identity, ["jr", "cd1"], ["jt"], bias=col(T.cd, 1))

    slot = {t: ((16 - t) // 4, (16 - t) % 4) for t in range(1, 16)}
    slot[8] = (0, 0)
    within = [T.lt[:, 4 * TILES[2]:4 * TILES[2] + 512:4], T.lt[:, 512:1024:4]]

    def lview(t):
        j, e = slot[t]
        return T.lt[:, 4 * TILES[j] + e:4 * TILES[j] + 64 * t:4]

    def lkeys(j):
        return ["l%d" % t for t in slot if slot[t][0] == j] + {0: ["dg1"], 2: ["dg0"]}.get(j, [])

    def wf(j, m=1):
        return T.wf[:, 16 * j:16 * (j + m)]

    def wi(j):
        return T.wi[:, 16 * j:16 * j + 16]

    def own_score(t):
        return col(T.sg, 16 * t + 15)

    def cmp(b, *blocks):
        for t in blocks:
            ts("c%d" % t, lview(t), bank(b, 0, 16 * t), own_score(t), None, A.is_lt, None,
               ["#%d" % b, "sg%d" % (t // 8), "z%d" % slot[t][0]], ["l%d" % t])

    def rows(*blocks):
        for t in blocks:
            act("rs", T.jk[:, 8 * t * (t - 1):8 * t * (t + 1)], lview(t), F.Identity, ["l%d" % t], ["rs%d" % t, "jk%d" % t],
                accum_out=col(T.rs, t))

    def cmp_rows(*blocks):
        signs = {t: T.sgn[:, 8 * t * (t - 1):8 * t * (t + 1)] for t in blocks}
        for t in blocks:
            act("sn%d" % t, signs[t], bank(1, 0, 16 * t), F.Sign, ["#1", "sg%d" % (t // 8)], ["sn%d" % t], scale=-1.0, bias=own_score(t))
        for t in blocks:
            act("rl%d" % (t // 8), lview(t), signs[t], F.Relu, ["sn%d" % t, "z%d" % slot[t][0]], ["l%d" % t, "rs%d" % t],
                accum_out=col(T.rs, t))

    def pack(tag, c, e, keys):
        quant(tag, T.ql[:, c:e], T.sl[:, c:e], T.lt[:, 4 * c:4 * e], keys, [tag])

    def count(tag, b, c, m, key, start=False, stop=False):
        mm(tag, bank(b, 0, m), T.qa[:], T.sa[:], T.ql[:, c:c + m], T.sl[:, c:c + m], [key, "qa"], ["#%d" % b], start=start, stop=stop)

    def lower_counts(first):
        pack("qlc", 512, 768 if first else 704, lkeys(2) + lkeys(3) + ["z4"])
        count("ml", 3, 512, 128, "qlc", start=True)
        count("ml", 3, 640, 128, "qlc")

    def upper_counts(first):
        pack("qlb", 256, 512 if first else 448, lkeys(1) + ["z5"])
        count("mh", 2, 256 + 128, 128, "qlb", start=True)
        count("ml", 3, 256, 128, "qlb")
        pack("qld", 128, 256, lkeys(0))
        count("mh", 2, 128, 128, "qld", stop=True)
        pack("qla", 0, 128, lkeys(0))
        count("ml", 3, 0, 128, "qla", stop=True)

    def offsets(h):
        scan("xv%d" % h, part(T.xv, h), part(T.jt, h), part(T.tc, h), A.max, A.mult, ["jt", "tc%d" % h], ["xv%d" % h])

    def scores(h):
        tt("sm%d" % h, part(T.sm, h), bank(3 - h, 0, 128), T.own[:], A.add, ["#%d" % (3 - h), "own"], ["sm%d" % h])

    def held_scores(h):
        hold("sg%d" % h, T.sg, T.d0g, T.sm, h, ["d0g", "sm%d" % h], ["sg%d" % h])

    def diagonal(h, b):
        tt("dg%d" % h, within[h], bank(b, 128 * h, 128 * h + 128), part(T.sg, h), A.is_le,
           ["#%d" % b, "sg%d" % h, "z%d" % (2 - 2 * h)], ["dg%d" % h])

    def diagonal_rows(h):
        scan("ds%d" % h, part(T.ds, h), T.d0d[:], within[h], A.mult, A.add, ["d0d", "dg%d" % h], ["ds%d" % h])

    qx, sx = T.qx[:], T.sx[:]
    QX = ["qx0", "qx1"]
    rid, pid = topo.addr(nxt)[:2]

    def colours():
        for j in range(2):
            mm("me%d" % j, bank(j), *side(T.qp, T.sp, 2 + j), qx, sx, QX + ["pc%d" % (2 + j), "ps%d" % (2 + j)], ["#%d" % j])
            act("eo%d" % j, part(T.eo, j, 256), bank(j), F.Sign, ["#%d" % j], ["eo%d" % j], bias=-TINY)

    def held_colours(*parts):
        for h in parts:
            hold("eh", T.eh, T.d0b, T.eo, h, ["d0b", "eo%d" % (h // 2)], ["eh%d" % h])

    def colour_scores(h):
        mm("m2", bank(2 - h, 0, 128), *side(T.qp, T.sp, 1), *side(T.qx, T.sx, h), ["qx%d" % h, "pc1", "ps1"], ["#%d" % (2 - h)])

    def served_colour(h):
        act("cs%d" % h, part(T.tc, h), bank(2 - h, 0, 128), F.Sign, ["#%d" % (2 - h), "cd2", "cd3"], ["tc%d" % h],
            scale=col(T.cd, 2), bias=col(T.cd, 3))

    def all_scores(b):
        mm("m%d" % b, bank(b), *side(T.qp, T.sp, 0), qx, sx, QX + ["pc0", "ps0"], ["#%d" % b])

    def half_scores(h, b):
        mm("ma%d" % b, bank(b, 0, 128), *side(T.qp, T.sp, 0), *side(T.qx, T.sx, h), ["qx%d" % h, "pc0", "ps0"], ["#%d" % b])

    def unpack():
        for b in range(4):
            mm("mf", bank(4 + b), *side(T.qe, T.se, b), qx, sx, QX + ["qe%d" % b], ["#%d" % (4 + b)])

    def window_list(*pieces):
        for h in pieces:
            m = min(128, 544 - 128 * h)
            scan("k20", T.tbh[:, 128 * h:128 * h + m], T.d0p[:, 0:m], T.tb[:, 128 * h:128 * h + m], A.add, A.max,
                 ["d0p"] + ["tb%d" % j for j in range(4)], ["tbh%d" % h])

    for k in range(ROUNDS):
        first, last = k == 0, k == ROUNDS - 1
        fused = 160 if last else 128
        if first:
            quant("qx1", *side(T.qx, T.sx, 1), part(T.xin, 1, 512), ["xin1"], ["qx1"])
            pick_codes(0)
            quant("qx0", *side(T.qx, T.sx, 0), part(T.xin, 0, 512), ["xin0"], ["qx0"])
            pick_codes(1)
            half_scores(1, 2)
            half_scores(0, 3)
            all_scores(0)
            all_scores(1)
            scores(1)
            scores(0)
            mm("m2", bank(2), *side(T.qp, T.sp, 1), qx, sx, QX + ["pc1", "ps1"], ["#2"])
            unit(3)
            unpack()
            held_scores(1)
            held_scores(0)
            cmp_rows(12, 11, 10)
            act("cs0", T.tc[:], bank(2), F.Sign, ["#2", "cd2", "cd3"], ["tc0", "tc1"], scale=col(T.cd, 2), bias=col(T.cd, 3))
            cmp(0, 15, 14)
            diagonal(0, 3)
            cmp(3, 7, 6, 5, 4, 3, 2, 1)
            rows(15, 14)
            cmp(0, 13)
            quant("qa", T.qa[:], T.sa[:], T.wab[:], ["wab%d" % j for j in range(4)], ["qa"])
            cmp(0, 9)
            lower_counts(first)
            diagonal(1, 0)
            cmp(0, 8)
            rows(7, 6, 5, 4, 3, 2, 1)
            rows(13, 9, 8)
        else:
            half_scores(1, 2)
            all_scores(0)
            held_scores(0)
            offsets(0)
            cmp(3, 5, 4, 3)
            cmp_rows(7, 6)
            all_scores(1)
            scores(1)
            unpack()
            cmp(3, 2, 1)
            diagonal(0, 3)
            held_scores(1)
            rows(5, 4, 3, 2, 1)
            cmp_rows(12, 11)
            colour_scores(1)
            lower_counts(first)
            cmp(0, 10, 9, 15, 14)
            rows(10, 9, 15, 14)
            cmp(0, 13)
            diagonal(1, 0)
            cmp(0, 8)
            rows(13, 8)
            served_colour(1)
        upper_counts(first)
        diagonal_rows(0)
        diagonal_rows(1)
        if first:
            offsets(0)
            act("k13", T.d0s[:], T.a16w[:, 0:280], F.Abs, ["a16w", "cf"], ["d0s"], scale=-1.0, bias=col(T.cf, PAR8))
            column("k14", 0, LAST, -2.0 * STEP, STEP)
            column("k14", 4, PAR8, -24.0 * STEP, 192.0 * STEP)
            column("k14", 11, PAR8, -96.0 * STEP, 0.0)
            column("k14", 6, R, 2.0, 34.5)
            column("k14", 7, R, 512.0, -7680.0)
            act("k15", col(T.d0s, 256), col(T.a16w, 0), F.Identity, ["d0s"], ["d0s"])
            act("k12", T.msel[:], T.m2[:], F.Identity, ["m2", "cd11"], ["msel"], scale=96.0 * STEP, bias=col(T.cd, 11))
            act("k16", T.d0s[:], T.d0s[:], F.Relu, ["d0s"], ["d0s"], scale=-1.0, bias=1.0)
            act("k21", col(T.msel, 31), col(T.cd, 0), F.Identity, ["cd0", "cd4", "msel"], ["msel"], scale=col(T.cf, PAR8), bias=col(T.cd, 4))
            act("k17", T.d0s[:], T.d0s[:], F.Identity, ["d0s", "cd0"], ["d0s"], scale=-2.0 ** 25, bias=col(T.cd, 0))
        tt("dc", T.pre[:, 0:16], T.ds[:, 15:256:16], T.kt[:], A.add, ["ds0", "ds1", "kt"], ["dc"])
        scan("hp1", part(T.hp, 1), T.d0p[:], bank(2, 0, 128), A.add, A.max, ["d0p", "#2"], ["hp1"])
        scan("hp0", part(T.hp, 0), T.d0p[:], bank(3, 0, 128), A.add, A.max, ["d0p", "#3"], ["hp0"])
        tt("pre", T.pre[:, 16:32], T.rs[:], T.pre[:, 0:16], A.add, ["dc"] + ["rs%d" % t for t in range(16)], ["pre"])
        offsets(1)
        tt("lp", T.lp[:], T.hp[:, 15:256:16], T.pre[:, 16:32], A.subtract, ["hp0", "hp1", "pre"], ["lp"])
        for b in (0, 2, 1, 3):
            o = 528 * (b % 2) + 1 + 257 * (b // 2)
            act("f%d" % (b % 2), T.f2[:, o:o + 256], bank(4 + b), F.Copy, ["#%d" % (4 + b)], ["f%d" % b])
        if not first:
            colours()
        cp("xo", T.xo[:, 0:256].indirect(T.lp[:]), T.xv[:], ["lp", "xv0", "xv1"], ["xo"])
        ts("w0", wi(0), T.lp[:], 248.0, None, A.add, None, ["lp"], ["w0"])
        scan("na", T.na[:, 256:280], T.d0s[:, 256:280], T.xo[:, 0:24], A.add, A.max, ["d0s", "xo"], ["nb"])
        scan("na", T.na[:, 0:256], T.d0s[:, 0:256], T.xo[:], A.add, A.max, ["d0s", "xo"], ["na"])
        ts("w1", wi(1), wi(0), 2, 62, A.logical_shift_right, A.bitwise_and, ["w0"], ["w1"])
        ts("w2", wi(2), wi(0), 3, 1, A.logical_shift_right, A.bitwise_and, ["w0"], ["w2"])
        for out in (T.s1, T.s2):
            scan("s1", out[:], T.msel[:], T.na[:, 15:280:8], A.add, A.max, ["na", "nb", "msel"], [out.name])
        ts("w3", wf(0), wi(1), col(T.cd, 6), None, A.add, None, ["w1", "cd6"], ["base"])
        tt("l1", T.l1[:, 0:17], T.s1[:, 1:34:2], T.s2[:, 1:34:2], A.subtract, ["s1", "s2"], ["l1"])
        ts("w4", wf(1), wi(2), 63.5, -31.5, A.mult, A.add, ["w2"], ["ce"])
        ts("w4", wf(2), wi(2), -63.5, 32.0, A.mult, A.add, ["w2"], ["co"])
        for h in range(2):
            act("g1%d" % h, part(T.gz, 2 + h, 144), T.f2[:, 528:1042].indirect(T.l1[:, 8 * h:8 * h + 9]), F.Copy,
                ["l1", "f1", "f3", "f2z"], ["g1%d" % h], scale=0.25)
            ts("g0%d" % h, part(T.gz, h, 144), T.f2[:, 0:514].indirect(T.l1[:, 8 * h:8 * h + 9]), 0.25, None, A.mult, None,
               ["l1", "f0", "f2", "f2y"], ["g0%d" % h])
        for h in range(2):
            for w in range(2):
                i = 2 * w + h
                scan("zz%d" % h, part(T.zz, i, 144), T.alt[:], part(T.gz, i, 144), A.mult, A.add, ["alt", "g%d%d" % (w, h)], ["zz%d" % i])
        for h in range(2):
            for w in range(2):
                i, m = 2 * w + h, 128 + 8 * h
                tt("y", T.yt[:, 128 * h + w:128 * h + m:2], T.zz[:, 144 * i + 1:144 * i + m:2], T.zz[:, 144 * i + 9:144 * i + 8 + m:2], A.add,
                   ["zz%d" % i], ["y%d" % i])
        if not first:
            held_colours(0, 1)
        quant("qy", *side(T.qy, T.sy, k), T.yt[:], ["y0", "y1", "y2", "y3", "ytz"], ["qy%d" % k])
        a, c = LAND[k], 128 * k
        arr = T.sem["arr%d" % k]
        op("g", None, lambda a=a, c=c, arr=arr: g.remote_dma(
            T.lc[:, a:a + NY].bitcast(dt.uint8), T.qy[:, c:c + NY].bitcast(dt.uint8), arr, T.sem.sent, pid, rid, topo.mask(core, nxt)), ["qy%d" % k])
        op("g", None, lambda a=a, c=c, arr=arr: g.remote_dma(
            T.ls[:, a:a + NY], T.sy[:, c:c + NY], arr, T.sem.sent, pid, rid, topo.mask(core, nxt)), [])
        if first:
            for j in range(3):
                iota("i13", part(T.ndt, j), [[1, 64], [j + 1, 2]], 0, 0, ["ndt%d" % j])
            iota("i14", T.ndt[:, 127:254:126], [[0, 2]], 0, 0, ["ndt0", "ndt1"])
            iota("i15", T.ndt[:, 255:382:126], [[0, 2]], 1, 0, ["ndt1", "ndt2"])
            pick_codes(2)
            pick_codes(3)
            window_list(0, 1, 2, 3, 4)
            pick_scales(2)
            pick_scales(3)
            act("k19", T.d0b[:], T.own[:], F.Identity, ["own"], ["d0b"], scale=-260.0 / BIG, bias=-256.0)
            act("k22", col(T.cd, 8), col(T.cf, COL4), F.Identity, ["cf"], ["cd8"], bias=col(T.cf, PAR8))
            column("k22", 10, R, 34.0, -1548.0)
            column("k22", 14, R, 4.0, -60.0)
            for h in range(2):
                blank("k23", part(T.zt, h, 256), 256, ["zt%d" % h])
            act("k24", T.a4[:], T.a4[:], F.Abs, ["a4", "cd8"], ["a4"], scale=-1.0, bias=col(T.cd, 8))
            act("k25", col(T.cd, 13), col(T.cd, 8), F.Identity, ["cd8", "cd10"], ["cd13"], scale=95.0, bias=col(T.cd, 10))
            blank("k25", T.ht[:, 264:512], 248, ["htz"])
            act("k26", T.a4[:], T.a4[:], F.Sign, ["a4"], ["a4"])
            colours()
            quant("lz", T.lc[:, 208:336], T.ls[:, 208:336], T.zt[:], ["zt0", "zt1"], ["lz"])
            ts("k28", T.lw[:], T.tbh[:, 15:544:16], col(T.cd, 7), None, A.add, None, ["cd7"] + ["tbh%d" % h for h in range(5)], ["lw"])
            held_colours(0, 1)
        held_colours(2, 3)
        for b in range(4):
            act("fi", T.fi[:, b:4 * fused:4], bank(4 + b, 0, fused), F.Copy, ["#%d" % (4 + b)], ["fi%d" % b])
        if first:
            act("k27", T.d0c[:], T.a4[:], F.Identity, ["a4"], ["d0c"], scale=260.0, bias=-256.0)
            act("k27", T.d0l[:], T.a4[:], F.Identity, ["a4"], ["d0l"], scale=66048.0, bias=-65536.0)
        tt("w5", wf(3, 2), T.eh[:, 15:512:16], wf(1, 2), A.mult, ["eh%d" % h for h in range(4)] + ["ce", "co"], ["w5"])
        if k == 1:
            quant("qv", T.qv[:], T.sv[:], T.vt[:], ["vt"], ["qv"])
        tt("w6", wf(5), wf(3), wf(0), A.add, ["w5", "base"], ["w6"])
        tt("w7", T.lcb[:], wf(5), wf(4), A.add, ["w5", "w6"], ["lcb"])
        act("lob", T.lob[:], T.ptab[:, 0:192].indirect(T.lcb[:]), F.Copy, ["lcb", "ptab0", "ptab1", "ptab2"], ["lob"])
        if last:
            ts("w8", wf(6), T.lcb[:], 2.0, col(T.cd, 14), A.mult, A.add, ["lcb", "cd14"], ["lo16"])
        got = (arr, 2 * len(topo.engines(prv, core)))
        for b in range(4):
            mm("mr%d" % b, bank(b, 0, 128), *side(T.qw, T.sw, b), T.lc[:, a:a + 128], T.ls[:, a:a + 128], ["qw", "sw", "lz"], ["#%d" % b],
               ext=got if b == 0 else None)
        for b in range(4):
            if b % 2 == 0:
                act("ha", T.ht[:, b:264:4], bank(b, 0, NY), F.Copy, ["#%d" % b], ["h%d" % b], scale=0.03125)
            else:
                ts("hv", T.ht[:, b:264:4], bank(b, 0, NY), 0.03125, None, A.mult, None, ["#%d" % b], ["h%d" % b])
        quant("qh", T.qh[:], T.sh[:], T.ht[:], ["h0", "h1", "h2", "h3", "htz"], ["qh"])
        act("th", T.th[:], T.nt[:, 0:192].indirect(T.lcb[:]), F.Relu, ["lcb", "nt"], ["th"], scale=TINY, bias=-61.5 * TINY)
        act("hw", T.hw[:], T.ht[:, 0:272].indirect(T.lw[:]), F.Copy, ["h0", "h1", "h2", "h3", "htz", "lw"], ["hw"])
        mm("mv", bank(0, 0, 128), *side(T.qp, T.sp, 0), T.qh[:], T.sh[:], ["qh"], ["#0"])
        for h in range(2):
            hold("l4", T.l4, T.d0l, T.lob, h, ["d0l", "lob"], ["l4%d" % h])
        cp("vs", T.vs[:], bank(0, 0, NY), ["#0"], ["vs"])
        ts("lo4", T.lo4[:], T.l4[:, 3:256:4], col(T.cd, 13), None, A.add, None, ["l40", "l41", "cd13"], ["lo4"])
        scan("d", T.dtb[:, 0:64], T.flip[:], bank(0, 1, 65), A.mult, A.subtract, ["#0", "flip"], ["d1"])
        tt("d", T.dtb[:, 64:128], T.vs[:, 0:64], bank(0, 2, 66), A.subtract, ["#0", "vs"], ["d2"])
        tt("d", T.dtb[:, 128:192:2], T.vs[:, 0:63:2], bank(0, 3, 66, 2), A.subtract, ["#0", "vs"], ["d3"])
        for h in range(2):
            tt("bt%d" % h, part(T.bt, h), T.dtb[:, 0:192].indirect(part(T.lcb, h, 8)), part(T.th, h), A.is_lt,
               ["d1", "d2", "d3", "lcb", "th"], ["bt%d" % h])
        for h in range(2):
            hold("bh%d" % h, T.bh, T.d0c, T.bt, h, ["d0c", "bt%d" % h], ["bh%d" % h])
            if last and h == 0:
                hold("b16", T.b16, T.d0b, T.bt, 0, ["bt0"], ["b160"])
        for h in range(2):
            tt("lh%d" % h, part(T.lh, h, 32), T.bh[:, 128 * h + 3:128 * h + 128:4], part(T.lo4, h, 32), A.add, ["bh%d" % h, "lo4"], ["lh%d" % h])
            if last and h == 0:
                hold("b16", T.b16, T.d0b, T.bt, 1, ["bt1"], ["b161"])
        cuts = [fused, 256] if last else [fused, 192, 256]
        for q in range(len(cuts) - 1):
            act("gh%d" % q, T.gh[:, 4 * cuts[q] - 512:4 * cuts[q + 1] - 512], T.hw[:, 0:544].indirect(T.lh[:, cuts[q] // 4:cuts[q + 1] // 4]),
                F.Copy, ["lh1", "hw"], ["gh%d" % q])
        FI = ["hw"] + ["fi%d" % b for b in range(4)]
        tt("xa", part(T.xs, 0, 512), T.hw[:, 0:544].indirect(part(T.lh, 0, 32)), T.fi[:, 0:512], A.add, ["lh0"] + FI, ["xa"])

        def rest(*pieces):
            for i in pieces:
                q, b = divmod(i, 4)
                c0, c1 = cuts[q], cuts[q + 1]
                tt("x", T.xs[:, 4 * c0 + b:4 * c1:4], bank(4 + b, c0, c1), T.gh[:, 4 * c0 - 512 + b:4 * c1 - 512:4],
                   A.add, ["#%d" % (4 + b), "gh%d" % q], ["x%d" % i])

        def packed(h):
            quant("qx%d" % h, *side(T.qx, T.sx, h), part(T.xs, h, 512), ["x%d" % b for b in range(8)] if h else ["xa"], ["qx%d" % h])
        if last:
            tt("ln", T.ln[:], T.b16[:, 15:256:16], wf(6), A.add, ["b160", "b161", "lo16"], ["ln"])
            act("nd", T.ndf[:], T.ndt[:, 0:384].indirect(T.ln[:]), F.Copy, ["ln", "ndt0", "ndt1", "ndt2"], ["ndf"])
            dma("a", "out", T.nd[:], T.ndf[0:128:16, :], ["ndf"], ["o0"])
            tt("x", T.xs[:, 512:4 * fused], T.hw[:, 0:544].indirect(T.lh[:, 32:fused // 4]), T.fi[:, 512:4 * fused], A.add, ["lh1"] + FI, ["x7"])
            rest(0, 1, 2, 3)
            packed(0)
            mm("ma3", bank(3, 0, 128), T.qv[:], T.sv[:], *side(T.qx, T.sx, 0), ["qx0", "qv"], ["#3"])
            packed(1)
        else:
            rest(0, 1)
            packed(0)
            half_scores(0, 3)
            colour_scores(0)
            half_scores(0, 1)
            served_colour(0)
            rest(2, 3, 4, 5, 6, 7)
            scores(0)
            packed(1)

    mm("m1", bank(1, 0, 128), T.qv[:], T.sv[:], *side(T.qx, T.sx, 1), ["qx1", "qv"], ["#1"])
    dma("s", "out", part(T.oc, 0, 512), part(T.qx, 0).bitcast(dt.uint8), ["qx0"], ["o1"])
    act("cs0", part(T.yo, 0), bank(3, 0, 128), F.Copy, ["#3"], ["yo0"])
    dma("a", "out", part(T.y, 0), part(T.yo, 0), ["yo0"], ["o2"])
    dma("s", "out", part(T.oc, 1, 512), part(T.qx, 1).bitcast(dt.uint8), ["qx1"], ["o3"])
    for j in range(4):
        dma("sa"[j // 3], "out", T.osc[4 * j:4 * j + 4, :], T.sx[32 * j:32 * j + 4, :], QX, ["o%d" % (4 + j)])
    cp("yo", part(T.yo, 1), bank(1, 0, 128), ["#1"], ["yo1"])
    dma("s", "out", part(T.y, 1), part(T.yo, 1), ["yo1"], ["o8"])
    op("g", None, None, ["o%d" % j for j in range(9)], ext=(T.sem.sent, 2 * ROUNDS * len(topo.engines(core, nxt))))

    sems, place = [], {}
    for tag, t in tags.items():
        raised = t["ops"][:t["closed"]]
        if not raised:
            continue
        bits, plain = sum(1 << o for o in raised), ops[raised[0]]["inc"] == 1
        free = [s for s in sems if plain and s["plain"] and s["bits"] & ~ops[raised[0]]["know"] == 0]
        if not free:
            free = [{"name": "s%d" % len(sems), "bits": 0, "sum": 0, "plain": plain}]
            sems.append(free[0])
        place[tag] = (T.sem[free[0]["name"]], free[0]["sum"])
        free[0]["bits"] |= bits
        free[0]["sum"] += sum(ops[o]["inc"] for o in raised)
    for i, o in enumerate(ops):
        if o["ext"]:
            queue[o["q"]].wait_ge(*o["ext"])
        for tag, val in o["waits"]:
            queue[o["q"]].wait_ge(place[tag][0], place[tag][1] + val)
        if o["fn"] is None:
            continue
        ins = o["fn"]()
        t = tags.get(o["tag"])
        if t and i in t["ops"][:t["closed"]]:
            ins.then_inc(place[o["tag"]][0], o["inc"])
